import numpy as np
import ml_dtypes


def mxq(x, axis, fmt="e4m3"):
    dtype, down = {"e4m3": (ml_dtypes.float8_e4m3fn, 7), "e5m2": (ml_dtypes.float8_e5m2, 14)}[fmt]
    v = np.moveaxis(np.asarray(x, np.float32).astype(ml_dtypes.bfloat16).astype(np.float64), axis, -1)
    blocks = v.reshape(v.shape[:-1] + (-1, 32))
    amax = np.abs(blocks).max(-1, keepdims=True)
    byte = np.maximum(np.where(amax > 0, np.frexp(amax)[1] - 1 + 127, 0) - down, 1)
    scale = np.exp2(byte - 127.0)
    codes = (blocks / scale).astype(np.float32).astype(dtype).astype(np.float64)
    return np.moveaxis((codes * scale).reshape(v.shape), -1, axis)


WIDE = False


def mx_kscale(k):
    if not WIDE:
        return np.ones(k)
    levels = np.array([10, -10, 5, -5, 0])
    if k % 512:
        return np.exp2(np.random.permutation(np.resize(levels, k // 32))).repeat(32)
    a = np.empty((k // 512, 16))
    for p in range(k // 512):
        a[p, :8] = np.random.permutation(np.resize(levels, 8))
        for g in range(8):
            far = levels[np.abs(levels - a[p, g]) >= 10]
            a[p, g + 8] = far[np.random.randint(len(far))]
    return np.exp2(a.ravel()).repeat(32)


def f64(x):
    return np.asarray(x).astype(np.float64)


def striped(idx):
    return np.tile(np.asarray(idx).reshape(-1, 16).T, (8, 1)).astype(np.uint16)


def unstriped(offs):
    return offs[:16].T.reshape(-1).astype(np.int64)


E2M1 = np.array([0.0, 0.5, 1.0, 1.5, 2.0, 3.0, 4.0, 6.0, -0.0, -0.5, -1.0, -1.5, -2.0, -3.0, -4.0, -6.0])


def pack_weight(w, fmt):
    k, n = w.shape
    w = f64(np.asarray(w, np.float32).astype(ml_dtypes.bfloat16)).reshape(k // 32, 32, n)
    amax = np.abs(w).max(1)
    if fmt == "e4m3":
        byte = np.frexp(amax)[1] - 1 + 127 - 7
    else:
        mant, ex = np.frexp(amax / 6.0)
        byte = np.where(mant > 0.5, ex, ex - 1) + 127
    byte = np.clip(np.where(amax > 0, byte, 1), 1, 254)
    scaled = (w * np.exp2(127.0 - byte)[:, None, :]).reshape(k, n).astype(np.float32)
    by_word = np.ascontiguousarray(scaled.reshape(k // 512, 128, 4, n).transpose(0, 1, 3, 2))
    if fmt == "e4m3":
        words = by_word.astype(ml_dtypes.float8_e4m3fn).view(np.uint8)
    else:
        c = by_word.astype(ml_dtypes.float4_e2m1fn).view(np.uint8) & 0xF
        words = (c[..., 0::2] | (c[..., 1::2] << 4)).reshape(k // 512, 128, 2 * n)
    return np.ascontiguousarray(words), np.ascontiguousarray(byte.astype(np.uint8).reshape(k // 512, 16, n))


def unpack_weight(words, scales, fmt):
    g, _, n = scales.shape
    words = np.ascontiguousarray(words).reshape(g, 128, n, -1)
    if fmt == "e4m3":
        vals = words.view(ml_dtypes.float8_e4m3fn).astype(np.float64)
    else:
        nib = np.empty((g, 128, n, 4), np.uint8)
        nib[..., 0::2] = words & 0xF
        nib[..., 1::2] = words >> 4
        vals = E2M1[nib]
    vals = vals * np.repeat(np.exp2(scales.astype(np.float64) - 127.0), 8, axis=1)[..., None]
    return vals.transpose(0, 1, 3, 2).reshape(g * 512, n)


B, N, T, D, DV, NQ = 1, 512, 2048, 1024, 128, 128


def setup_inputs():
    n = np.random.standard_normal
    idx = np.random.permutation(T)[:B * N]
    s = mx_kscale(D)[:, None]
    u = np.ones(T)
    u[idx] = mx_kscale(B * N)
    r = np.random.uniform(0.5, 2.0, T)
    k = n((D, T)) / s
    v = n((DV, T)) / (u * r)
    kp = pack_weight(k, "e2m1")
    return {
        "qT": (n((B, D, NQ)) * s * (1.00 / np.sqrt(D))).astype(np.float32),
        "k_words": np.ascontiguousarray(kp[0].reshape(D // 1024, 2, 128, T, 2).transpose(0, 2, 3, 1, 4)).reshape(D // 1024, 128, T, 4),
        "k_scales": kp[1],
        "vT": v.astype(np.float32),
        "vs": np.tile(u * r, (128, 1)).astype(np.float32),
        "kb": np.tile(n(T), (128, 1)).astype(np.float32),
        "offs": striped(idx),
    }


def reference(qT, k_words, k_scales, vT, vs, kb, offs):
    idx = unstriped(offs)
    k = unpack_weight(k_words.reshape(D // 1024, 128, T, 2, 2).transpose(0, 3, 1, 2, 4).reshape(D // 512, 128, 2 * T), k_scales, "e2m1")
    v = f64(vT)
    pick = lambda x: x[:, idx].reshape(x.shape[0], B, N).transpose(1, 0, 2)
    q = f64(qT)
    score = mxq(q, 1, "e4m3").transpose(0, 2, 1) @ pick(k)
    score = score + pick(f64(kb))[:, :1, :]
    p = score / (1.0 + np.exp(-score))
    w = p * pick(f64(vs))[:, :1, :]
    y = mxq(w, 2, "e4m3") @ mxq(pick(v).transpose(0, 2, 1), 1, "e4m3")
    y = y / 16.0
    return y

@@ -1,0 +1,154 @@
+from contextlib import ExitStack
+
+import concourse.mybir as mybir
+from concourse.masks import make_identity
+
+D, T, N, NQ, DV = 1024, 2048, 512, 128, 128
+FLOPS = 2 * NQ * N * (D + DV)
+BYTES = 4 * D * NQ + 4 * 128 * T + 2 * 16 * T + 4 * DV * T + 2 * 4 * T + 2 * 128 * (N // 16) + 4 * NQ * DV
+
+F32 = mybir.dt.float32
+BF16 = mybir.dt.bfloat16
+I32 = mybir.dt.int32
+U32 = mybir.dt.uint32
+U16 = mybir.dt.uint16
+U8 = mybir.dt.uint8
+FP8X4 = mybir.dt.float8_e4m3fn_x4
+FP4X4 = mybir.dt.float4_e2m1fn_x4
+ACT = mybir.ActivationFunctionType
+MULT = mybir.AluOpType.mult
+
+P = 128
+PACK = 4
+PASSES = D // (P * PACK)
+KB_ROW = 8
+VS_ROW = 16
+SCALE_ROW = 96
+
+
+def slot_order(ap):
+    return ap.rearrange("p t (j r) -> p j t r", r=8)
+
+
+def tile_attend_silu_kb_topkq128n512t2048_kernel(tc, qT, k_words, k_scales, vT, vs, kb, offs, out):
+    nc = tc.nc
+    with ExitStack() as ctx:
+        sb = ctx.enter_context(tc.tile_pool(name="sb", bufs=1))
+        ps = ctx.enter_context(tc.psum_pool(name="ps", bufs=1))
+
+        offsets = sb.tile([P, N // 16], U16, name="offsets")
+        nc.sync.dma_start(offsets[:], offs)
+        scale_pool = sb.tile([P, T], U8, name="scale_pool", align_bytes=64)
+        nc.sync.dma_start(scale_pool[SCALE_ROW:, :].bitcast(I32), k_scales.rearrange("o f t -> (o f) t").bitcast(I32))
+
+        word_pool = sb.tile([P, T], I32, name="word_pool")
+        nc.scalar.dma_start(word_pool[:], k_words[0].rearrange("p t b -> p (t b)").bitcast(I32))
+        q_raw = sb.tile([P, PASSES, PACK, NQ], F32, name="q_raw")
+        nc.scalar.dma_start(q_raw[:], qT[0].rearrange("(o p t) n -> p o t n", o=PASSES, t=PACK))
+        v_pool = sb.tile([P, T], F32, name="v_pool")
+        nc.scalar.dma_start(v_pool[:], vT)
+
+        kb_pool = sb.tile([P, T], F32, name="kb_pool")
+        vs_pool = sb.tile([P, T], F32, name="vs_pool")
+        k_scale = sb.tile([P, PASSES, N], U8, name="k_scale", align_bytes=64)
+        nc.vector.memset(kb_pool[:], 0.0)
+        nc.vector.memset(scale_pool[:SCALE_ROW, :].bitcast(I32), 0)
+        nc.vector.memset(vs_pool[:], 0.0)
+        nc.vector.memset(k_scale[:].rearrange("p o n -> p (o n)").bitcast(I32), 0)
+        nc.sync.dma_start(kb_pool[KB_ROW : KB_ROW + 1, :], kb[0:1, :])
+        nc.sync.dma_start(vs_pool[VS_ROW : VS_ROW + 1, :], vs[0:1, :])
+
+        ident = sb.tile([P, P], F32, name="ident")
+        make_identity(nc, ident[:])
+
+        q_bf = sb.tile([P, PASSES, NQ, PACK], BF16, name="q_bf", align_bytes=64)
+        nc.scalar.activation(q_bf[:], q_raw[:].rearrange("p o t n -> p o n t"), ACT.Copy)
+
+        scale_picked = sb.tile([P, N], U8, name="scale_picked", align_bytes=64)
+        nc.vector.tensor_copy(scale_picked[:], scale_pool[:].indirect(offsets[:]))
+        scale_sorted = sb.tile([P, N], U8, name="scale_sorted", align_bytes=64)
+        nc.vector.tensor_copy(
+            scale_sorted[:].bitcast(I32).rearrange("p (t j c) -> p t j c", t=PACK, c=2),
+            scale_picked[:].bitcast(I32).rearrange("p (j t c) -> p t j c", t=PACK, c=2),
+        )
+        for o in range(PASSES):
+            for quad in range(4):
+                src = SCALE_ROW + 16 * o + 4 * quad
+                nc.sync.dma_start(
+                    k_scale[32 * quad : 32 * quad + 4, o, :].bitcast(I32),
+                    scale_sorted[src : src + 4, :].bitcast(I32),
+                )
+
+        words = sb.tile([P, N], U32, name="words")
+        nc.vector.tensor_copy(words[:], word_pool[:].bitcast(U32).indirect(offsets[:]))
+
+        def slot_columns(pool, row, name):
+            picked = sb.tile([P, PACK, P], F32, name=name + "_picked")
+            nc.vector.tensor_copy(slot_order(picked[:].bitcast(U32)), pool[:].bitcast(U32).indirect(offsets[:]))
+            turned = ps.tile([P, PACK, P], F32, name=name + "_turned")
+            for t in range(PACK):
+                nc.tensor.transpose(turned[:, t, :], picked[:, t, :], ident[:])
+            col = sb.tile([P, PACK], F32, name=name + "_col")
+            nc.scalar.copy(col[:], turned[:, :, row])
+            return col
+
+        kb_col = slot_columns(kb_pool, KB_ROW, "kb")
+        vs_col = slot_columns(vs_pool, VS_ROW, "vs")
+
+        q_codes = sb.tile([P, PASSES * NQ], U32, name="q_codes", align_bytes=64)
+        q_scale = sb.tile([P, PASSES * NQ], U8, name="q_scale", align_bytes=64)
+        nc.vector.quantize_mx(out=q_codes[:].bitcast(FP8X4), scales=q_scale[:], in_=q_bf[:].rearrange("p o n t -> p (o n t)"))
+
+        halves = words[:].bitcast(U16).rearrange("p (j t r o) -> p t o j r", t=PACK, r=8, o=PASSES)
+        p_all = sb.tile([P, PACK, NQ], F32, name="p_all")
+        for u in range(2):
+            k_codes = sb.tile([P, 2, PASSES, P], U16, name="k_codes%d" % u, align_bytes=64)
+            nc.vector.tensor_copy(k_codes[:].rearrange("p e o (j r) -> p e o j r", r=8), halves[:, 2 * u : 2 * u + 2])
+            for e in range(2):
+                t = 2 * u + e
+                acc = ps.tile([P, NQ], F32, name="scores%d" % t)
+                for o in range(PASSES):
+                    nc.tensor.matmul_mx(
+                        out=acc[:],
+                        lhsT=k_codes[:, e, o, :].bitcast(FP4X4),
+                        lhsT_scale=k_scale[:, o, t * P : (t + 1) * P],
+                        rhs=q_codes[:, o * NQ : (o + 1) * NQ].bitcast(FP8X4),
+                        rhs_scale=q_scale[:, o * NQ : (o + 1) * NQ],
+                        start=(o == 0),
+                        stop=(o == PASSES - 1),
+                    )
+                nc.scalar.activation(p_all[:, t, :], acc[:], ACT.Silu, bias=kb_col[:, t : t + 1])
+
+        v_picked = sb.tile([P, 2, P, 2], BF16, name="v_picked")
+        nc.vector.tensor_copy(v_picked[:].rearrange("p u (j r) e -> p j u e r", r=8), v_pool[:].indirect(offsets[:]))
+        v_turned = ps.tile([P, 2, DV], F32, name="v_turned")
+        for u in range(2):
+            nc.tensor.transpose(v_turned[:, u, :], v_picked[:, u].rearrange("p m e -> p (m e)").bitcast(F32), ident[:])
+        v_bf = sb.tile([P, DV * PACK], BF16, name="v_bf", align_bytes=64)
+        nc.scalar.copy(v_bf[:].bitcast(F32).rearrange("p (c u) -> p c u", u=2), v_turned[:].rearrange("p u c -> p c u"))
+
+        w_bf = sb.tile([P, NQ, PACK], BF16, name="w_bf", align_bytes=64)
+        nc.vector.tensor_tensor(
+            w_bf[:], p_all[:].rearrange("p t q -> p q t"), vs_col[:].unsqueeze(1).to_broadcast([P, NQ, PACK]), MULT
+        )
+
+        v_codes = sb.tile([P, DV], U32, name="v_codes", align_bytes=64)
+        v_scale = sb.tile([P, DV], U8, name="v_scale", align_bytes=64)
+        nc.vector.quantize_mx(out=v_codes[:].bitcast(FP8X4), scales=v_scale[:], in_=v_bf[:])
+        w_codes = sb.tile([P, NQ], U32, name="w_codes", align_bytes=64)
+        w_scale = sb.tile([P, NQ], U8, name="w_scale", align_bytes=64)
+        nc.vector.quantize_mx(out=w_codes[:].bitcast(FP8X4), scales=w_scale[:], in_=w_bf[:].rearrange("p q t -> p (q t)"))
+
+        y_acc = ps.tile([NQ, DV], F32, name="y_acc")
+        nc.tensor.matmul_mx(
+            out=y_acc[:],
+            lhsT=w_codes[:].bitcast(FP8X4),
+            lhsT_scale=w_scale[:],
+            rhs=v_codes[:].bitcast(FP8X4),
+            rhs_scale=v_scale[:],
+            start=True,
+            stop=True,
+        )
+        y = sb.tile([NQ, DV], F32, name="y")
+        nc.vector.tensor_scalar(y[:], y_acc[:], 1.0 / 16.0, None, MULT)
+        nc.sync.dma_start(out[0], y[:])

@@ -23,7 +23,6 @@ PACK = 4
 PASSES = D // (P * PACK)
 KB_ROW = 8
 VS_ROW = 16
-SCALE_ROW = 96
 
 
 def slot_order(ap):
@@ -38,64 +37,75 @@ def tile_attend_silu_kb_topkq128n512t2048_kernel(tc, qT, k_words, k_scales, vT, 
 
         offsets = sb.tile([P, N // 16], U16, name="offsets")
         nc.sync.dma_start(offsets[:], offs)
-        scale_pool = sb.tile([P, T], U8, name="scale_pool", align_bytes=64)
-        nc.sync.dma_start(scale_pool[SCALE_ROW:, :].bitcast(I32), k_scales.rearrange("o f t -> (o f) t").bitcast(I32))
+        scale_pool = sb.tile([P, T], U8, name="scale_pool", tag="scales_then_v", align_bytes=64)
+        nc.sync.dma_start(scale_pool[:32, :].bitcast(I32), k_scales.rearrange("o f t -> (o f) t").bitcast(I32))
 
-        word_pool = sb.tile([P, T], I32, name="word_pool")
-        nc.scalar.dma_start(word_pool[:], k_words[0].rearrange("p t b -> p (t b)").bitcast(I32))
         q_raw = sb.tile([P, PASSES, PACK, NQ], F32, name="q_raw")
         nc.scalar.dma_start(q_raw[:], qT[0].rearrange("(o p t) n -> p o t n", o=PASSES, t=PACK))
-        v_pool = sb.tile([P, T], F32, name="v_pool")
-        nc.scalar.dma_start(v_pool[:], vT)
+        word_pool = sb.tile([P, T], I32, name="word_pool", tag="words_then_q", align_bytes=64)
+        nc.scalar.dma_start(word_pool[:], k_words[0].rearrange("p t b -> p (t b)").bitcast(I32))
 
-        kb_pool = sb.tile([P, T], F32, name="kb_pool")
-        vs_pool = sb.tile([P, T], F32, name="vs_pool")
-        k_scale = sb.tile([P, PASSES, N], U8, name="k_scale", align_bytes=64)
-        nc.vector.memset(kb_pool[:], 0.0)
-        nc.vector.memset(scale_pool[:SCALE_ROW, :].bitcast(I32), 0)
-        nc.vector.memset(vs_pool[:], 0.0)
-        nc.vector.memset(k_scale[:].rearrange("p o n -> p (o n)").bitcast(I32), 0)
+        kb_pool = sb.tile([P, T], F32, name="kb_pool", tag="kb_words_vs")
+        vs_pool = sb.tile([P, T], F32, name="vs_pool", tag="vs_then_v")
+        plane1 = sb.tile([P, N], U8, name="plane1", align_bytes=64)
+        nc.gpsimd.memset(scale_pool[32:64, :].bitcast(I32), 0)
+        nc.vector.memset(kb_pool[:].bitcast(I32), 0)
         nc.sync.dma_start(kb_pool[KB_ROW : KB_ROW + 1, :], kb[0:1, :])
+        nc.vector.memset(scale_pool[64:, :].bitcast(I32), 0)
+        nc.vector.memset(plane1[:].bitcast(I32), 0)
+        nc.vector.memset(vs_pool[:].bitcast(I32), 0)
         nc.sync.dma_start(vs_pool[VS_ROW : VS_ROW + 1, :], vs[0:1, :])
 
-        ident = sb.tile([P, P], F32, name="ident")
-        make_identity(nc, ident[:])
-
-        q_bf = sb.tile([P, PASSES, NQ, PACK], BF16, name="q_bf", align_bytes=64)
-        nc.scalar.activation(q_bf[:], q_raw[:].rearrange("p o t n -> p o n t"), ACT.Copy)
-
-        scale_picked = sb.tile([P, N], U8, name="scale_picked", align_bytes=64)
+        scale_picked = sb.tile([P, N], U8, name="scale_picked", tag="scales_then_ident", align_bytes=64)
         nc.vector.tensor_copy(scale_picked[:], scale_pool[:].indirect(offsets[:]))
-        scale_sorted = sb.tile([P, N], U8, name="scale_sorted", align_bytes=64)
+        v_pool = sb.tile([P, T], F32, name="v_pool", tag="scales_then_v", align_bytes=64)
+        nc.scalar.dma_start(v_pool[:], vT)
+        plane0 = sb.tile([P, N], U8, name="plane0", align_bytes=64)
         nc.vector.tensor_copy(
-            scale_sorted[:].bitcast(I32).rearrange("p (t j c) -> p t j c", t=PACK, c=2),
+            plane0[:].bitcast(I32).rearrange("p (t j c) -> p t j c", t=PACK, c=2),
             scale_picked[:].bitcast(I32).rearrange("p (j t c) -> p t j c", t=PACK, c=2),
         )
+        k_scale = [plane0, plane1]
         for o in range(PASSES):
             for quad in range(4):
-                src = SCALE_ROW + 16 * o + 4 * quad
-                nc.sync.dma_start(
-                    k_scale[32 * quad : 32 * quad + 4, o, :].bitcast(I32),
-                    scale_sorted[src : src + 4, :].bitcast(I32),
-                )
+                src = 16 * o + 4 * quad
+                if src > 0:
+                    nc.sync.dma_start(
+                        k_scale[o][32 * quad : 32 * quad + 4, :].bitcast(I32),
+                        plane0[src : src + 4, :].bitcast(I32),
+                    )
 
-        words = sb.tile([P, N], U32, name="words")
-        nc.vector.tensor_copy(words[:], word_pool[:].bitcast(U32).indirect(offsets[:]))
+        warm_in = sb.tile([P, 1], F32, name="warm_in")
+        nc.gpsimd.memset(warm_in[:], 0.0)
+        warm_out = sb.tile([P, 1], F32, name="warm_out", tag="warm_then_q", align_bytes=64)
+        nc.scalar.activation(warm_out[:], warm_in[:], ACT.Silu)
+        q_bf = sb.tile([P, PASSES, NQ, PACK], BF16, name="q_bf", tag="warm_then_q", align_bytes=64)
+        for o in range(PASSES):
+            nc.scalar.activation(
+                q_bf[:, o].rearrange("p (c i) t -> p c t i", i=4),
+                q_raw[:, o].rearrange("p t (c i) -> p c t i", i=4),
+                ACT.Copy,
+            )
 
-        def slot_columns(pool, row, name):
-            picked = sb.tile([P, PACK, P], F32, name=name + "_picked")
+        ident = sb.tile([P, P], F32, name="ident", tag="scales_then_ident", align_bytes=64)
+        make_identity(nc, ident[:])
+
+        def slot_columns(pool, row, name, picked_tag, bank):
+            picked = sb.tile([P, PACK, P], F32, name=name + "_picked", tag=picked_tag)
             nc.vector.tensor_copy(slot_order(picked[:].bitcast(U32)), pool[:].bitcast(U32).indirect(offsets[:]))
-            turned = ps.tile([P, PACK, P], F32, name=name + "_turned")
+            turned = ps.tile([P, PACK, P], F32, name=name + "_turned", tag=bank)
             for t in range(PACK):
                 nc.tensor.transpose(turned[:, t, :], picked[:, t, :], ident[:])
             col = sb.tile([P, PACK], F32, name=name + "_col")
             nc.scalar.copy(col[:], turned[:, :, row])
             return col
 
-        kb_col = slot_columns(kb_pool, KB_ROW, "kb")
-        vs_col = slot_columns(vs_pool, VS_ROW, "vs")
+        kb_col = slot_columns(kb_pool, KB_ROW, "kb", "kb_picked", "bank0")
 
-        q_codes = sb.tile([P, PASSES * NQ], U32, name="q_codes", align_bytes=64)
+        words = sb.tile([P, N], U32, name="words", tag="kb_words_vs")
+        nc.vector.tensor_copy(words[:], word_pool[:].bitcast(U32).indirect(offsets[:]))
+
+        q_codes = sb.tile([P, PASSES * NQ], U32, name="q_codes", tag="words_then_q", align_bytes=64)
         q_scale = sb.tile([P, PASSES * NQ], U8, name="q_scale", align_bytes=64)
         nc.vector.quantize_mx(out=q_codes[:].bitcast(FP8X4), scales=q_scale[:], in_=q_bf[:].rearrange("p o n t -> p (o n t)"))
 
@@ -106,12 +116,12 @@ def tile_attend_silu_kb_topkq128n512t2048_kernel(tc, qT, k_words, k_scales, vT, 
             nc.vector.tensor_copy(k_codes[:].rearrange("p e o (j r) -> p e o j r", r=8), halves[:, 2 * u : 2 * u + 2])
             for e in range(2):
                 t = 2 * u + e
-                acc = ps.tile([P, NQ], F32, name="scores%d" % t)
+                acc = ps.tile([P, NQ], F32, name="scores%d" % t, tag="bank%d" % t)
                 for o in range(PASSES):
                     nc.tensor.matmul_mx(
                         out=acc[:],
                         lhsT=k_codes[:, e, o, :].bitcast(FP4X4),
-                        lhsT_scale=k_scale[:, o, t * P : (t + 1) * P],
+                        lhsT_scale=k_scale[o][:, t * P : (t + 1) * P],
                         rhs=q_codes[:, o * NQ : (o + 1) * NQ].bitcast(FP8X4),
                         rhs_scale=q_scale[:, o * NQ : (o + 1) * NQ],
                         start=(o == 0),
@@ -119,9 +129,11 @@ def tile_attend_silu_kb_topkq128n512t2048_kernel(tc, qT, k_words, k_scales, vT, 
                     )
                 nc.scalar.activation(p_all[:, t, :], acc[:], ACT.Silu, bias=kb_col[:, t : t + 1])
 
-        v_picked = sb.tile([P, 2, P, 2], BF16, name="v_picked")
+        vs_col = slot_columns(vs_pool, VS_ROW, "vs", "kb_words_vs", "bank0")
+
+        v_picked = sb.tile([P, 2, P, 2], BF16, name="v_picked", tag="vs_then_v")
         nc.vector.tensor_copy(v_picked[:].rearrange("p u (j r) e -> p j u e r", r=8), v_pool[:].indirect(offsets[:]))
-        v_turned = ps.tile([P, 2, DV], F32, name="v_turned")
+        v_turned = ps.tile([P, 2, DV], F32, name="v_turned", tag="bank1")
         for u in range(2):
             nc.tensor.transpose(v_turned[:, u, :], v_picked[:, u].rearrange("p m e -> p (m e)").bitcast(F32), ident[:])
         v_bf = sb.tile([P, DV * PACK], BF16, name="v_bf", align_bytes=64)

@@ -45,12 +45,12 @@ def tile_attend_silu_kb_topkq128n512t2048_kernel(tc, qT, k_words, k_scales, vT, 
         word_pool = sb.tile([P, T], I32, name="word_pool", tag="words_then_q", align_bytes=64)
         nc.scalar.dma_start(word_pool[:], k_words[0].rearrange("p t b -> p (t b)").bitcast(I32))
 
-        kb_pool = sb.tile([P, T], F32, name="kb_pool", tag="kb_words_vs")
-        vs_pool = sb.tile([P, T], F32, name="vs_pool", tag="vs_then_v")
+        kb_pool = sb.tile([P, T], F32, name="kb_pool", tag="kb_words_v")
+        vs_pool = sb.tile([P, T], F32, name="vs_pool", tag="vs_then_keys", align_bytes=64)
         plane1 = sb.tile([P, N], U8, name="plane1", align_bytes=64)
-        nc.gpsimd.memset(scale_pool[32:64, :].bitcast(I32), 0)
         nc.vector.memset(kb_pool[:].bitcast(I32), 0)
         nc.sync.dma_start(kb_pool[KB_ROW : KB_ROW + 1, :], kb[0:1, :])
+        nc.vector.memset(scale_pool[32:64, :].bitcast(I32), 0)
         nc.vector.memset(scale_pool[64:, :].bitcast(I32), 0)
         nc.vector.memset(plane1[:].bitcast(I32), 0)
         nc.vector.memset(vs_pool[:].bitcast(I32), 0)
@@ -90,20 +90,27 @@ def tile_attend_silu_kb_topkq128n512t2048_kernel(tc, qT, k_words, k_scales, vT, 
         ident = sb.tile([P, P], F32, name="ident", tag="scales_then_ident", align_bytes=64)
         make_identity(nc, ident[:])
 
-        def slot_columns(pool, row, name, picked_tag, bank):
-            picked = sb.tile([P, PACK, P], F32, name=name + "_picked", tag=picked_tag)
+        def pick(pool, name):
+            picked = sb.tile([P, PACK, P], F32, name=name)
             nc.vector.tensor_copy(slot_order(picked[:].bitcast(U32)), pool[:].bitcast(U32).indirect(offsets[:]))
-            turned = ps.tile([P, PACK, P], F32, name=name + "_turned", tag=bank)
-            for t in range(PACK):
-                nc.tensor.transpose(turned[:, t, :], picked[:, t, :], ident[:])
-            col = sb.tile([P, PACK], F32, name=name + "_col")
-            nc.scalar.copy(col[:], turned[:, :, row])
-            return col
+            return picked
 
-        kb_col = slot_columns(kb_pool, KB_ROW, "kb", "kb_picked", "bank0")
+        kb_picked = pick(kb_pool, "kb_picked")
+        kb_col = sb.tile([P, PACK], F32, name="kb_col")
+        for t in range(PACK):
+            kb_turned = ps.tile([P, P], F32, name="kb_turned%d" % t, tag="bank%d" % t)
+            nc.tensor.transpose(kb_turned[:], kb_picked[:, t, :], ident[:])
+            nc.scalar.copy(kb_col[:, t : t + 1], kb_turned[:, KB_ROW : KB_ROW + 1])
 
-        words = sb.tile([P, N], U32, name="words", tag="kb_words_vs")
+        words = sb.tile([P, N], U32, name="words", tag="kb_words_v")
         nc.vector.tensor_copy(words[:], word_pool[:].bitcast(U32).indirect(offsets[:]))
+
+        vs_picked = pick(vs_pool, "vs_picked")
+        vs_turned = ps.tile([P, PACK, P], F32, name="vs_turned")
+        for t in range(PACK):
+            nc.tensor.transpose(vs_turned[:, t, :], vs_picked[:, t, :], ident[:])
+        vs_col = sb.tile([P, PACK], F32, name="vs_col")
+        nc.scalar.copy(vs_col[:], vs_turned[:, :, VS_ROW])
 
         q_codes = sb.tile([P, PASSES * NQ], U32, name="q_codes", tag="words_then_q", align_bytes=64)
         q_scale = sb.tile([P, PASSES * NQ], U8, name="q_scale", align_bytes=64)
@@ -111,16 +118,17 @@ def tile_attend_silu_kb_topkq128n512t2048_kernel(tc, qT, k_words, k_scales, vT, 
 
         halves = words[:].bitcast(U16).rearrange("p (j t r o) -> p t o j r", t=PACK, r=8, o=PASSES)
         p_all = sb.tile([P, PACK, NQ], F32, name="p_all")
+        k_codes = sb.tile([P, PACK, PASSES, P], U16, name="k_codes", tag="vs_then_keys", align_bytes=64)
         for u in range(2):
-            k_codes = sb.tile([P, 2, PASSES, P], U16, name="k_codes%d" % u, align_bytes=64)
-            nc.vector.tensor_copy(k_codes[:].rearrange("p e o (j r) -> p e o j r", r=8), halves[:, 2 * u : 2 * u + 2])
+            pair = slice(2 * u, 2 * u + 2)
+            nc.vector.tensor_copy(k_codes[:, pair].rearrange("p e o (j r) -> p e o j r", r=8), halves[:, pair])
             for e in range(2):
                 t = 2 * u + e
                 acc = ps.tile([P, NQ], F32, name="scores%d" % t, tag="bank%d" % t)
                 for o in range(PASSES):
                     nc.tensor.matmul_mx(
                         out=acc[:],
-                        lhsT=k_codes[:, e, o, :].bitcast(FP4X4),
+                        lhsT=k_codes[:, t, o, :].bitcast(FP4X4),
                         lhsT_scale=k_scale[o][:, t * P : (t + 1) * P],
                         rhs=q_codes[:, o * NQ : (o + 1) * NQ].bitcast(FP8X4),
                         rhs_scale=q_scale[:, o * NQ : (o + 1) * NQ],
@@ -129,20 +137,17 @@ def tile_attend_silu_kb_topkq128n512t2048_kernel(tc, qT, k_words, k_scales, vT, 
                     )
                 nc.scalar.activation(p_all[:, t, :], acc[:], ACT.Silu, bias=kb_col[:, t : t + 1])
 
-        vs_col = slot_columns(vs_pool, VS_ROW, "vs", "kb_words_vs", "bank0")
-
-        v_picked = sb.tile([P, 2, P, 2], BF16, name="v_picked", tag="vs_then_v")
+        v_picked = sb.tile([P, 2, P, 2], BF16, name="v_picked", tag="kb_words_v")
         nc.vector.tensor_copy(v_picked[:].rearrange("p u (j r) e -> p j u e r", r=8), v_pool[:].indirect(offsets[:]))
-        v_turned = ps.tile([P, 2, DV], F32, name="v_turned", tag="bank1")
+        v_turned = ps.tile([P, 2, DV], F32, name="v_turned")
         for u in range(2):
             nc.tensor.transpose(v_turned[:, u, :], v_picked[:, u].rearrange("p m e -> p (m e)").bitcast(F32), ident[:])
         v_bf = sb.tile([P, DV * PACK], BF16, name="v_bf", align_bytes=64)
         nc.scalar.copy(v_bf[:].bitcast(F32).rearrange("p (c u) -> p c u", u=2), v_turned[:].rearrange("p u c -> p c u"))
 
         w_bf = sb.tile([P, NQ, PACK], BF16, name="w_bf", align_bytes=64)
-        nc.vector.tensor_tensor(
-            w_bf[:], p_all[:].rearrange("p t q -> p q t"), vs_col[:].unsqueeze(1).to_broadcast([P, NQ, PACK]), MULT
-        )
+        for t in range(PACK):
+            nc.vector.tensor_scalar(w_bf[:, :, t], p_all[:, t, :], vs_col[:, t : t + 1], None, MULT)
 
         v_codes = sb.tile([P, DV], U32, name="v_codes", align_bytes=64)
         v_scale = sb.tile([P, DV], U8, name="v_scale", align_bytes=64)

@@ -37,16 +37,16 @@ def tile_attend_silu_kb_topkq128n512t2048_kernel(tc, qT, k_words, k_scales, vT, 
 
         offsets = sb.tile([P, N // 16], U16, name="offsets")
         nc.sync.dma_start(offsets[:], offs)
-        scale_pool = sb.tile([P, T], U8, name="scale_pool", tag="scales_then_v", align_bytes=64)
+        scale_pool = sb.tile([P, T], U8, name="scale_pool", align_bytes=64)
         nc.sync.dma_start(scale_pool[:32, :].bitcast(I32), k_scales.rearrange("o f t -> (o f) t").bitcast(I32))
 
-        q_raw = sb.tile([P, PASSES, PACK, NQ], F32, name="q_raw")
+        q_raw = sb.tile([P, PASSES, PACK, NQ], F32, name="q_raw", tag="q_then_ident")
         nc.scalar.dma_start(q_raw[:], qT[0].rearrange("(o p t) n -> p o t n", o=PASSES, t=PACK))
         word_pool = sb.tile([P, T], I32, name="word_pool", tag="words_then_q", align_bytes=64)
         nc.scalar.dma_start(word_pool[:], k_words[0].rearrange("p t b -> p (t b)").bitcast(I32))
 
-        kb_pool = sb.tile([P, T], F32, name="kb_pool", tag="kb_words_v")
-        vs_pool = sb.tile([P, T], F32, name="vs_pool", tag="vs_then_keys", align_bytes=64)
+        kb_pool = sb.tile([P, T], F32, name="kb_pool", tag="kb_then_vs")
+        vs_pool = sb.tile([P, T], F32, name="vs_pool", tag="vs_words_v")
         plane1 = sb.tile([P, N], U8, name="plane1", align_bytes=64)
         nc.vector.memset(kb_pool[:].bitcast(I32), 0)
         nc.sync.dma_start(kb_pool[KB_ROW : KB_ROW + 1, :], kb[0:1, :])
@@ -56,10 +56,8 @@ def tile_attend_silu_kb_topkq128n512t2048_kernel(tc, qT, k_words, k_scales, vT, 
         nc.vector.memset(vs_pool[:].bitcast(I32), 0)
         nc.sync.dma_start(vs_pool[VS_ROW : VS_ROW + 1, :], vs[0:1, :])
 
-        scale_picked = sb.tile([P, N], U8, name="scale_picked", tag="scales_then_ident", align_bytes=64)
+        scale_picked = sb.tile([P, N], U8, name="scale_picked", tag="scales_then_v", align_bytes=64)
         nc.vector.tensor_copy(scale_picked[:], scale_pool[:].indirect(offsets[:]))
-        v_pool = sb.tile([P, T], F32, name="v_pool", tag="scales_then_v", align_bytes=64)
-        nc.scalar.dma_start(v_pool[:], vT)
         plane0 = sb.tile([P, N], U8, name="plane0", align_bytes=64)
         nc.vector.tensor_copy(
             plane0[:].bitcast(I32).rearrange("p (t j c) -> p t j c", t=PACK, c=2),
@@ -74,6 +72,8 @@ def tile_attend_silu_kb_topkq128n512t2048_kernel(tc, qT, k_words, k_scales, vT, 
                         k_scale[o][32 * quad : 32 * quad + 4, :].bitcast(I32),
                         plane0[src : src + 4, :].bitcast(I32),
                     )
+        v_pool = sb.tile([P, T], F32, name="v_pool", tag="scales_then_v", align_bytes=64)
+        nc.sync.dma_start(v_pool[:], vT)
 
         warm_in = sb.tile([P, 1], F32, name="warm_in")
         nc.gpsimd.memset(warm_in[:], 0.0)
@@ -87,30 +87,30 @@ def tile_attend_silu_kb_topkq128n512t2048_kernel(tc, qT, k_words, k_scales, vT, 
                 ACT.Copy,
             )
 
-        ident = sb.tile([P, P], F32, name="ident", tag="scales_then_ident", align_bytes=64)
+        ident = sb.tile([P, P], F32, name="ident", tag="q_then_ident")
         make_identity(nc, ident[:])
 
-        def pick(pool, name):
-            picked = sb.tile([P, PACK, P], F32, name=name)
+        def pick(pool, name, tag):
+            picked = sb.tile([P, PACK, P], F32, name=name, tag=tag)
             nc.vector.tensor_copy(slot_order(picked[:].bitcast(U32)), pool[:].bitcast(U32).indirect(offsets[:]))
             return picked
 
-        kb_picked = pick(kb_pool, "kb_picked")
+        kb_picked = pick(kb_pool, "kb_picked", "kb_picked")
         kb_col = sb.tile([P, PACK], F32, name="kb_col")
         for t in range(PACK):
             kb_turned = ps.tile([P, P], F32, name="kb_turned%d" % t, tag="bank%d" % t)
             nc.tensor.transpose(kb_turned[:], kb_picked[:, t, :], ident[:])
             nc.scalar.copy(kb_col[:, t : t + 1], kb_turned[:, KB_ROW : KB_ROW + 1])
 
-        words = sb.tile([P, N], U32, name="words", tag="kb_words_v")
-        nc.vector.tensor_copy(words[:], word_pool[:].bitcast(U32).indirect(offsets[:]))
-
-        vs_picked = pick(vs_pool, "vs_picked")
-        vs_turned = ps.tile([P, PACK, P], F32, name="vs_turned")
+        vs_picked = pick(vs_pool, "vs_picked", "kb_then_vs")
+        vs_turned = ps.tile([P, PACK, P], F32, name="vs_turned", tag="bank0")
         for t in range(PACK):
             nc.tensor.transpose(vs_turned[:, t, :], vs_picked[:, t, :], ident[:])
         vs_col = sb.tile([P, PACK], F32, name="vs_col")
         nc.scalar.copy(vs_col[:], vs_turned[:, :, VS_ROW])
+
+        words = sb.tile([P, N], U32, name="words", tag="vs_words_v")
+        nc.vector.tensor_copy(words[:], word_pool[:].bitcast(U32).indirect(offsets[:]))
 
         q_codes = sb.tile([P, PASSES * NQ], U32, name="q_codes", tag="words_then_q", align_bytes=64)
         q_scale = sb.tile([P, PASSES * NQ], U8, name="q_scale", align_bytes=64)
@@ -118,7 +118,7 @@ def tile_attend_silu_kb_topkq128n512t2048_kernel(tc, qT, k_words, k_scales, vT, 
 
         halves = words[:].bitcast(U16).rearrange("p (j t r o) -> p t o j r", t=PACK, r=8, o=PASSES)
         p_all = sb.tile([P, PACK, NQ], F32, name="p_all")
-        k_codes = sb.tile([P, PACK, PASSES, P], U16, name="k_codes", tag="vs_then_keys", align_bytes=64)
+        k_codes = sb.tile([P, PACK, PASSES, P], U16, name="k_codes", align_bytes=64)
         for u in range(2):
             pair = slice(2 * u, 2 * u + 2)
             nc.vector.tensor_copy(k_codes[:, pair].rearrange("p e o (j r) -> p e o j r", r=8), halves[:, pair])
@@ -137,15 +137,15 @@ def tile_attend_silu_kb_topkq128n512t2048_kernel(tc, qT, k_words, k_scales, vT, 
                     )
                 nc.scalar.activation(p_all[:, t, :], acc[:], ACT.Silu, bias=kb_col[:, t : t + 1])
 
-        v_picked = sb.tile([P, 2, P, 2], BF16, name="v_picked", tag="kb_words_v")
+        v_picked = sb.tile([P, 2, P, 2], BF16, name="v_picked", tag="vs_words_v")
         nc.vector.tensor_copy(v_picked[:].rearrange("p u (j r) e -> p j u e r", r=8), v_pool[:].indirect(offsets[:]))
-        v_turned = ps.tile([P, 2, DV], F32, name="v_turned")
+        v_turned = ps.tile([P, 2, DV], F32, name="v_turned", tag="bank2")
         for u in range(2):
             nc.tensor.transpose(v_turned[:, u, :], v_picked[:, u].rearrange("p m e -> p (m e)").bitcast(F32), ident[:])
         v_bf = sb.tile([P, DV * PACK], BF16, name="v_bf", align_bytes=64)
         nc.scalar.copy(v_bf[:].bitcast(F32).rearrange("p (c u) -> p c u", u=2), v_turned[:].rearrange("p u c -> p c u"))
 
-        w_bf = sb.tile([P, NQ, PACK], BF16, name="w_bf", align_bytes=64)
+        w_bf = sb.tile([P, NQ, PACK], BF16, name="w_bf", tag="scales_then_v", align_bytes=64)
         for t in range(PACK):
             nc.vector.tensor_scalar(w_bf[:, :, t], p_all[:, t, :], vs_col[:, t : t + 1], None, MULT)
 

@@ -22,7 +22,7 @@ P = 128
 PACK = 4
 PASSES = D // (P * PACK)
 KB_ROW = 8
-VS_ROW = 16
+RUN = T // P
 
 
 def slot_order(ap):
@@ -37,26 +37,41 @@ def tile_attend_silu_kb_topkq128n512t2048_kernel(tc, qT, k_words, k_scales, vT, 
 
         offsets = sb.tile([P, N // 16], U16, name="offsets")
         nc.sync.dma_start(offsets[:], offs)
-        scale_pool = sb.tile([P, T], U8, name="scale_pool", align_bytes=64)
+        scale_pool = sb.tile([P, T], U8, name="scale_pool", tag="scales_then_kb", align_bytes=64)
         nc.sync.dma_start(scale_pool[:32, :].bitcast(I32), k_scales.rearrange("o f t -> (o f) t").bitcast(I32))
+        vs_runs = sb.tile([P, RUN], F32, name="vs_runs")
+        nc.sync.dma_start(vs_runs[:], vs[0].rearrange("(p j) -> p j", j=RUN))
 
-        q_raw = sb.tile([P, PASSES, PACK, NQ], F32, name="q_raw", tag="q_then_ident")
+        q_raw = sb.tile([P, PASSES, PACK, NQ], F32, name="q_raw", tag="q_then_v")
         nc.scalar.dma_start(q_raw[:], qT[0].rearrange("(o p t) n -> p o t n", o=PASSES, t=PACK))
-        word_pool = sb.tile([P, T], I32, name="word_pool", tag="words_then_q", align_bytes=64)
+        word_pool = sb.tile([P, T], I32, name="word_pool", tag="words_then_vs", align_bytes=64)
         nc.scalar.dma_start(word_pool[:], k_words[0].rearrange("p t b -> p (t b)").bitcast(I32))
 
-        kb_pool = sb.tile([P, T], F32, name="kb_pool", tag="kb_then_vs")
-        vs_pool = sb.tile([P, T], F32, name="vs_pool", tag="vs_words_v")
+        kb_pool = sb.tile([P, T], F32, name="kb_pool", tag="kb_then_q", align_bytes=64)
         plane1 = sb.tile([P, N], U8, name="plane1", align_bytes=64)
         nc.vector.memset(kb_pool[:].bitcast(I32), 0)
         nc.sync.dma_start(kb_pool[KB_ROW : KB_ROW + 1, :], kb[0:1, :])
         nc.vector.memset(scale_pool[32:64, :].bitcast(I32), 0)
         nc.vector.memset(scale_pool[64:, :].bitcast(I32), 0)
         nc.vector.memset(plane1[:].bitcast(I32), 0)
-        nc.vector.memset(vs_pool[:].bitcast(I32), 0)
-        nc.sync.dma_start(vs_pool[VS_ROW : VS_ROW + 1, :], vs[0:1, :])
 
-        scale_picked = sb.tile([P, N], U8, name="scale_picked", tag="scales_then_v", align_bytes=64)
+        warm_in = sb.tile([P, 1], F32, name="warm_in")
+        nc.gpsimd.memset(warm_in[:], 0.0)
+        ident = sb.tile([P, P], F32, name="ident")
+        make_identity(nc, ident[:])
+        warm_out = sb.tile([P, 1], F32, name="warm_out", tag="warm_then_q", align_bytes=64)
+        nc.scalar.activation(warm_out[:], warm_in[:], ACT.Silu)
+        q_bf = sb.tile([P, PASSES, NQ, PACK], BF16, name="q_bf", tag="warm_then_q", align_bytes=64)
+        for o in range(PASSES):
+            nc.scalar.activation(
+                q_bf[:, o].rearrange("p (c i) t -> p c t i", i=4),
+                q_raw[:, o].rearrange("p t (c i) -> p c t i", i=4),
+                ACT.Copy,
+            )
+        v_pool = sb.tile([P, T], F32, name="v_pool", tag="q_then_v")
+        nc.scalar.dma_start(v_pool[:], vT)
+
+        scale_picked = sb.tile([P, N], U8, name="scale_picked", align_bytes=64)
         nc.vector.tensor_copy(scale_picked[:], scale_pool[:].indirect(offsets[:]))
         plane0 = sb.tile([P, N], U8, name="plane0", align_bytes=64)
         nc.vector.tensor_copy(
@@ -72,47 +87,33 @@ def tile_attend_silu_kb_topkq128n512t2048_kernel(tc, qT, k_words, k_scales, vT, 
                         k_scale[o][32 * quad : 32 * quad + 4, :].bitcast(I32),
                         plane0[src : src + 4, :].bitcast(I32),
                     )
-        v_pool = sb.tile([P, T], F32, name="v_pool", tag="scales_then_v", align_bytes=64)
-        nc.sync.dma_start(v_pool[:], vT)
 
-        warm_in = sb.tile([P, 1], F32, name="warm_in")
-        nc.gpsimd.memset(warm_in[:], 0.0)
-        warm_out = sb.tile([P, 1], F32, name="warm_out", tag="warm_then_q", align_bytes=64)
-        nc.scalar.activation(warm_out[:], warm_in[:], ACT.Silu)
-        q_bf = sb.tile([P, PASSES, NQ, PACK], BF16, name="q_bf", tag="warm_then_q", align_bytes=64)
-        for o in range(PASSES):
-            nc.scalar.activation(
-                q_bf[:, o].rearrange("p (c i) t -> p c t i", i=4),
-                q_raw[:, o].rearrange("p t (c i) -> p c t i", i=4),
-                ACT.Copy,
+        vs_pool = sb.tile([P, T], F32, name="vs_pool")
+        for b in range(RUN // 4):
+            spread = ps.tile([P, 4, P], F32, name="spread%d" % b, tag="bank%d" % b)
+            for j in range(4):
+                nc.tensor.transpose(spread[:, j, :], vs_runs[:, 4 * b + j : 4 * b + j + 1].to_broadcast([P, P]), ident[:])
+            nc.scalar.copy(
+                vs_pool[:].rearrange("p (m b j) -> p b m j", b=RUN // 4, j=4)[:, b],
+                spread[:].rearrange("p j m -> p m j"),
             )
 
-        ident = sb.tile([P, P], F32, name="ident", tag="q_then_ident")
-        make_identity(nc, ident[:])
-
         def pick(pool, name, tag):
-            picked = sb.tile([P, PACK, P], F32, name=name, tag=tag)
+            picked = sb.tile([P, PACK, P], F32, name=name, tag=tag, align_bytes=64)
             nc.vector.tensor_copy(slot_order(picked[:].bitcast(U32)), pool[:].bitcast(U32).indirect(offsets[:]))
             return picked
 
-        kb_picked = pick(kb_pool, "kb_picked", "kb_picked")
+        kb_picked = pick(kb_pool, "kb_picked", "scales_then_kb")
+        kb_turned = ps.tile([P, PACK, P], F32, name="kb_turned")
+        for t in range(PACK):
+            nc.tensor.transpose(kb_turned[:, t, :], kb_picked[:, t, :], ident[:])
         kb_col = sb.tile([P, PACK], F32, name="kb_col")
-        for t in range(PACK):
-            kb_turned = ps.tile([P, P], F32, name="kb_turned%d" % t, tag="bank%d" % t)
-            nc.tensor.transpose(kb_turned[:], kb_picked[:, t, :], ident[:])
-            nc.scalar.copy(kb_col[:, t : t + 1], kb_turned[:, KB_ROW : KB_ROW + 1])
+        nc.scalar.copy(kb_col[:], kb_turned[:, :, KB_ROW])
 
-        vs_picked = pick(vs_pool, "vs_picked", "kb_then_vs")
-        vs_turned = ps.tile([P, PACK, P], F32, name="vs_turned", tag="bank0")
-        for t in range(PACK):
-            nc.tensor.transpose(vs_turned[:, t, :], vs_picked[:, t, :], ident[:])
-        vs_col = sb.tile([P, PACK], F32, name="vs_col")
-        nc.scalar.copy(vs_col[:], vs_turned[:, :, VS_ROW])
-
-        words = sb.tile([P, N], U32, name="words", tag="vs_words_v")
+        words = sb.tile([P, N], U32, name="words", tag="words_then_v")
         nc.vector.tensor_copy(words[:], word_pool[:].bitcast(U32).indirect(offsets[:]))
 
-        q_codes = sb.tile([P, PASSES * NQ], U32, name="q_codes", tag="words_then_q", align_bytes=64)
+        q_codes = sb.tile([P, PASSES * NQ], U32, name="q_codes", tag="kb_then_q", align_bytes=64)
         q_scale = sb.tile([P, PASSES * NQ], U8, name="q_scale", align_bytes=64)
         nc.vector.quantize_mx(out=q_codes[:].bitcast(FP8X4), scales=q_scale[:], in_=q_bf[:].rearrange("p o n t -> p (o n t)"))
 
@@ -137,24 +138,35 @@ def tile_attend_silu_kb_topkq128n512t2048_kernel(tc, qT, k_words, k_scales, vT, 
                     )
                 nc.scalar.activation(p_all[:, t, :], acc[:], ACT.Silu, bias=kb_col[:, t : t + 1])
 
-        v_picked = sb.tile([P, 2, P, 2], BF16, name="v_picked", tag="vs_words_v")
+        vs_picked = pick(vs_pool, "vs_picked", "words_then_vs")
+        vs_turned = ps.tile([P, PACK, P], F32, name="vs_turned")
+        for t in range(PACK):
+            nc.tensor.transpose(vs_turned[:, t, :], vs_picked[:, t, :], ident[:])
+        vs_col = sb.tile([P, PACK], F32, name="vs_col")
+        nc.scalar.copy(vs_col[:], vs_turned[:, :, 0])
+
+        v_picked = sb.tile([P, 2, P, 2], BF16, name="v_picked", tag="words_then_v")
         nc.vector.tensor_copy(v_picked[:].rearrange("p u (j r) e -> p j u e r", r=8), v_pool[:].indirect(offsets[:]))
-        v_turned = ps.tile([P, 2, DV], F32, name="v_turned", tag="bank2")
+        v_turned = ps.tile([P, 2, DV], F32, name="v_turned")
         for u in range(2):
             nc.tensor.transpose(v_turned[:, u, :], v_picked[:, u].rearrange("p m e -> p (m e)").bitcast(F32), ident[:])
         v_bf = sb.tile([P, DV * PACK], BF16, name="v_bf", align_bytes=64)
         nc.scalar.copy(v_bf[:].bitcast(F32).rearrange("p (c u) -> p c u", u=2), v_turned[:].rearrange("p u c -> p c u"))
 
-        w_bf = sb.tile([P, NQ, PACK], BF16, name="w_bf", tag="scales_then_v", align_bytes=64)
-        for t in range(PACK):
-            nc.vector.tensor_scalar(w_bf[:, :, t], p_all[:, t, :], vs_col[:, t : t + 1], None, MULT)
+        w_bf = sb.tile([P, NQ, PACK], BF16, name="w_bf", align_bytes=64)
+        nc.vector.tensor_tensor(
+            w_bf[:].rearrange("p (c i) t -> p c t i", i=4),
+            p_all[:].rearrange("p t (c i) -> p c t i", i=4),
+            vs_col[:].unsqueeze(1).unsqueeze(3).to_broadcast([P, NQ // 4, PACK, 4]),
+            MULT,
+        )
 
-        v_codes = sb.tile([P, DV], U32, name="v_codes", align_bytes=64)
-        v_scale = sb.tile([P, DV], U8, name="v_scale", align_bytes=64)
-        nc.vector.quantize_mx(out=v_codes[:].bitcast(FP8X4), scales=v_scale[:], in_=v_bf[:])
         w_codes = sb.tile([P, NQ], U32, name="w_codes", align_bytes=64)
         w_scale = sb.tile([P, NQ], U8, name="w_scale", align_bytes=64)
         nc.vector.quantize_mx(out=w_codes[:].bitcast(FP8X4), scales=w_scale[:], in_=w_bf[:].rearrange("p q t -> p (q t)"))
+        v_codes = sb.tile([P, DV], U32, name="v_codes", align_bytes=64)
+        v_scale = sb.tile([P, DV], U8, name="v_scale", align_bytes=64)
+        nc.vector.quantize_mx(out=v_codes[:].bitcast(FP8X4), scales=v_scale[:], in_=v_bf[:])
 
         y_acc = ps.tile([NQ, DV], F32, name="y_acc")
         nc.tensor.matmul_mx(

@@ -38,57 +38,47 @@ def tile_attend_silu_kb_topkq128n512t2048_kernel(tc, qT, k_words, k_scales, vT, 
         offsets = sb.tile([P, N // 16], U16, name="offsets")
         nc.sync.dma_start(offsets[:], offs)
         scale_pool = sb.tile([P, T], U8, name="scale_pool", tag="scales_then_kb", align_bytes=64)
-        nc.sync.dma_start(scale_pool[:32, :].bitcast(I32), k_scales.rearrange("o f t -> (o f) t").bitcast(I32))
+        nc.sync.dma_start(scale_pool[:32, :].bitcast(I32), k_scales.rearrange("o f t -> f o t").bitcast(I32))
         vs_runs = sb.tile([P, RUN], F32, name="vs_runs")
         nc.sync.dma_start(vs_runs[:], vs[0].rearrange("(p j) -> p j", j=RUN))
 
-        q_raw = sb.tile([P, PASSES, PACK, NQ], F32, name="q_raw", tag="q_then_v")
-        nc.scalar.dma_start(q_raw[:], qT[0].rearrange("(o p t) n -> p o t n", o=PASSES, t=PACK))
         word_pool = sb.tile([P, T], I32, name="word_pool", tag="words_then_vs", align_bytes=64)
-        nc.scalar.dma_start(word_pool[:], k_words[0].rearrange("p t b -> p (t b)").bitcast(I32))
+        nc.sync.dma_start(word_pool[:], k_words[0].rearrange("p t b -> p (t b)").bitcast(I32))
+        q_raw = [sb.tile([P, PACK, NQ], F32, name="q_raw%d" % o) for o in range(PASSES)]
+        for o in range(PASSES):
+            nc.sync.dma_start(q_raw[o][:], qT[0].rearrange("(o p t) n -> o p t n", o=PASSES, t=PACK)[o])
 
         kb_pool = sb.tile([P, T], F32, name="kb_pool", tag="kb_then_q", align_bytes=64)
-        plane1 = sb.tile([P, N], U8, name="plane1", align_bytes=64)
+        planes = sb.tile([P, PASSES, N], U8, name="planes", align_bytes=64)
         nc.vector.memset(kb_pool[:].bitcast(I32), 0)
-        nc.sync.dma_start(kb_pool[KB_ROW : KB_ROW + 1, :], kb[0:1, :])
+        nc.scalar.dma_start(kb_pool[KB_ROW : KB_ROW + 1, :], kb[0:1, :])
         nc.vector.memset(scale_pool[32:64, :].bitcast(I32), 0)
         nc.vector.memset(scale_pool[64:, :].bitcast(I32), 0)
-        nc.vector.memset(plane1[:].bitcast(I32), 0)
+        nc.vector.memset(planes[:].bitcast(I32), 0)
 
         warm_in = sb.tile([P, 1], F32, name="warm_in")
         nc.gpsimd.memset(warm_in[:], 0.0)
         ident = sb.tile([P, P], F32, name="ident")
         make_identity(nc, ident[:])
-        warm_out = sb.tile([P, 1], F32, name="warm_out", tag="warm_then_q", align_bytes=64)
+        warm_out = sb.tile([P, 1], F32, name="warm_out", tag="warm_then_vs", align_bytes=64)
         nc.scalar.activation(warm_out[:], warm_in[:], ACT.Silu)
-        q_bf = sb.tile([P, PASSES, NQ, PACK], BF16, name="q_bf", tag="warm_then_q", align_bytes=64)
-        for o in range(PASSES):
-            nc.scalar.activation(
-                q_bf[:, o].rearrange("p (c i) t -> p c t i", i=4),
-                q_raw[:, o].rearrange("p t (c i) -> p c t i", i=4),
-                ACT.Copy,
-            )
-        v_pool = sb.tile([P, T], F32, name="v_pool", tag="q_then_v")
-        nc.scalar.dma_start(v_pool[:], vT)
 
-        scale_picked = sb.tile([P, N], U8, name="scale_picked", align_bytes=64)
+        scale_picked = sb.tile([P, N], U8, name="scale_picked", tag="scales_then_v", align_bytes=64)
         nc.vector.tensor_copy(scale_picked[:], scale_pool[:].indirect(offsets[:]))
-        plane0 = sb.tile([P, N], U8, name="plane0", align_bytes=64)
+        scale_sorted = sb.tile([P, N], U8, name="scale_sorted", align_bytes=64)
         nc.vector.tensor_copy(
-            plane0[:].bitcast(I32).rearrange("p (t j c) -> p t j c", t=PACK, c=2),
+            scale_sorted[:].bitcast(I32).rearrange("p (t j c) -> p t j c", t=PACK, c=2),
             scale_picked[:].bitcast(I32).rearrange("p (j t c) -> p t j c", t=PACK, c=2),
         )
-        k_scale = [plane0, plane1]
-        for o in range(PASSES):
-            for quad in range(4):
-                src = 16 * o + 4 * quad
-                if src > 0:
-                    nc.sync.dma_start(
-                        k_scale[o][32 * quad : 32 * quad + 4, :].bitcast(I32),
-                        plane0[src : src + 4, :].bitcast(I32),
-                    )
+        for quad in range(4):
+            nc.sync.dma_start(
+                planes[32 * quad : 32 * quad + 4].bitcast(I32),
+                scale_sorted[8 * quad : 8 * quad + 8, :].bitcast(I32),
+            )
+        v_pool = sb.tile([P, T], F32, name="v_pool", tag="scales_then_v", align_bytes=64)
+        nc.sync.dma_start(v_pool[:], vT)
 
-        vs_pool = sb.tile([P, T], F32, name="vs_pool")
+        vs_pool = sb.tile([P, T], F32, name="vs_pool", tag="warm_then_vs", align_bytes=64)
         for b in range(RUN // 4):
             spread = ps.tile([P, 4, P], F32, name="spread%d" % b, tag="bank%d" % b)
             for j in range(4):
@@ -96,6 +86,14 @@ def tile_attend_silu_kb_topkq128n512t2048_kernel(tc, qT, k_words, k_scales, vT, 
             nc.scalar.copy(
                 vs_pool[:].rearrange("p (m b j) -> p b m j", b=RUN // 4, j=4)[:, b],
                 spread[:].rearrange("p j m -> p m j"),
+            )
+
+        q_bf = sb.tile([P, PASSES, NQ, PACK], BF16, name="q_bf", align_bytes=64)
+        for o in range(PASSES):
+            nc.scalar.activation(
+                q_bf[:, o].rearrange("p (c i) t -> p c t i", i=4),
+                q_raw[o][:].rearrange("p t (c i) -> p c t i", i=4),
+                ACT.Copy,
             )
 
         def pick(pool, name, tag):
@@ -130,7 +128,7 @@ def tile_attend_silu_kb_topkq128n512t2048_kernel(tc, qT, k_words, k_scales, vT, 
                     nc.tensor.matmul_mx(
                         out=acc[:],
                         lhsT=k_codes[:, t, o, :].bitcast(FP4X4),
-                        lhsT_scale=k_scale[o][:, t * P : (t + 1) * P],
+                        lhsT_scale=planes[:, o, t * P : (t + 1) * P],
                         rhs=q_codes[:, o * NQ : (o + 1) * NQ].bitcast(FP8X4),
                         rhs_scale=q_scale[:, o * NQ : (o + 1) * NQ],
                         start=(o == 0),

@@ -22,6 +22,7 @@ P = 128
 PACK = 4
 PASSES = D // (P * PACK)
 KB_ROW = 8
+SCALE_ROW = 96
 RUN = T // P
 
 
@@ -33,34 +34,33 @@ def tile_attend_silu_kb_topkq128n512t2048_kernel(tc, qT, k_words, k_scales, vT, 
     nc = tc.nc
     with ExitStack() as ctx:
         sb = ctx.enter_context(tc.tile_pool(name="sb", bufs=1))
+        reuse = ctx.enter_context(tc.tile_pool(name="reuse", bufs=1))
         ps = ctx.enter_context(tc.psum_pool(name="ps", bufs=1))
 
         offsets = sb.tile([P, N // 16], U16, name="offsets")
         nc.sync.dma_start(offsets[:], offs)
-        scale_pool = sb.tile([P, T], U8, name="scale_pool", tag="scales_then_kb", align_bytes=64)
-        nc.sync.dma_start(scale_pool[:32, :].bitcast(I32), k_scales.rearrange("o f t -> f o t").bitcast(I32))
-        vs_runs = sb.tile([P, RUN], F32, name="vs_runs")
+        scale_pool = sb.tile([P, T], U8, name="scale_pool")
+        nc.sync.dma_start(scale_pool[SCALE_ROW:, :].bitcast(I32), k_scales.rearrange("o f t -> f o t").bitcast(I32))
+        vs_runs = sb.tile([P, RUN], F32, name="vs_runs", tag="runs_then_q", align_bytes=64)
         nc.sync.dma_start(vs_runs[:], vs[0].rearrange("(p j) -> p j", j=RUN))
 
-        word_pool = sb.tile([P, T], I32, name="word_pool", tag="words_then_vs", align_bytes=64)
+        word_pool = sb.tile([P, T], I32, name="word_pool", tag="words_then_kb")
         nc.sync.dma_start(word_pool[:], k_words[0].rearrange("p t b -> p (t b)").bitcast(I32))
-        q_raw = [sb.tile([P, PACK, NQ], F32, name="q_raw%d" % o) for o in range(PASSES)]
-        for o in range(PASSES):
-            nc.sync.dma_start(q_raw[o][:], qT[0].rearrange("(o p t) n -> o p t n", o=PASSES, t=PACK)[o])
+        q_raw = reuse.tile([P, PASSES, PACK, NQ], F32, name="q_raw", offset=0)
+        nc.sync.dma_start(q_raw[:], qT[0].rearrange("(o p t) n -> p o t n", o=PASSES, t=PACK))
 
         kb_pool = sb.tile([P, T], F32, name="kb_pool", tag="kb_then_q", align_bytes=64)
         planes = sb.tile([P, PASSES, N], U8, name="planes", align_bytes=64)
         nc.vector.memset(kb_pool[:].bitcast(I32), 0)
         nc.scalar.dma_start(kb_pool[KB_ROW : KB_ROW + 1, :], kb[0:1, :])
-        nc.vector.memset(scale_pool[32:64, :].bitcast(I32), 0)
-        nc.vector.memset(scale_pool[64:, :].bitcast(I32), 0)
+        nc.vector.memset(scale_pool[:SCALE_ROW, :].bitcast(I32), 0)
         nc.vector.memset(planes[:].bitcast(I32), 0)
 
         warm_in = sb.tile([P, 1], F32, name="warm_in")
         nc.gpsimd.memset(warm_in[:], 0.0)
         ident = sb.tile([P, P], F32, name="ident")
         make_identity(nc, ident[:])
-        warm_out = sb.tile([P, 1], F32, name="warm_out", tag="warm_then_vs", align_bytes=64)
+        warm_out = sb.tile([P, 1], F32, name="warm_out", tag="warm_then_vs")
         nc.scalar.activation(warm_out[:], warm_in[:], ACT.Silu)
 
         scale_picked = sb.tile([P, N], U8, name="scale_picked", tag="scales_then_v", align_bytes=64)
@@ -73,12 +73,12 @@ def tile_attend_silu_kb_topkq128n512t2048_kernel(tc, qT, k_words, k_scales, vT, 
         for quad in range(4):
             nc.sync.dma_start(
                 planes[32 * quad : 32 * quad + 4].bitcast(I32),
-                scale_sorted[8 * quad : 8 * quad + 8, :].bitcast(I32),
+                scale_sorted[SCALE_ROW + 8 * quad : SCALE_ROW + 8 * quad + 8, :].bitcast(I32),
             )
         v_pool = sb.tile([P, T], F32, name="v_pool", tag="scales_then_v", align_bytes=64)
         nc.sync.dma_start(v_pool[:], vT)
 
-        vs_pool = sb.tile([P, T], F32, name="vs_pool", tag="warm_then_vs", align_bytes=64)
+        vs_pool = sb.tile([P, T], F32, name="vs_pool", tag="warm_then_vs")
         for b in range(RUN // 4):
             spread = ps.tile([P, 4, P], F32, name="spread%d" % b, tag="bank%d" % b)
             for j in range(4):
@@ -88,64 +88,62 @@ def tile_attend_silu_kb_topkq128n512t2048_kernel(tc, qT, k_words, k_scales, vT, 
                 spread[:].rearrange("p j m -> p m j"),
             )
 
-        q_bf = sb.tile([P, PASSES, NQ, PACK], BF16, name="q_bf", align_bytes=64)
+        q_bf = sb.tile([P, PASSES, NQ, PACK], BF16, name="q_bf", tag="runs_then_q", align_bytes=64)
         for o in range(PASSES):
             nc.scalar.activation(
                 q_bf[:, o].rearrange("p (c i) t -> p c t i", i=4),
-                q_raw[o][:].rearrange("p t (c i) -> p c t i", i=4),
+                q_raw[:, o].rearrange("p t (c i) -> p c t i", i=4),
                 ACT.Copy,
             )
 
-        def pick(pool, name, tag):
-            picked = sb.tile([P, PACK, P], F32, name=name, tag=tag, align_bytes=64)
+        def pick(picked, pool):
             nc.vector.tensor_copy(slot_order(picked[:].bitcast(U32)), pool[:].bitcast(U32).indirect(offsets[:]))
-            return picked
 
-        kb_picked = pick(kb_pool, "kb_picked", "scales_then_kb")
+        words = sb.tile([P, N], U32, name="words")
+        nc.vector.tensor_copy(words[:], word_pool[:].bitcast(U32).indirect(offsets[:]))
+
+        halves = words[:].bitcast(U16).rearrange("p (j t r o) -> p t o j r", t=PACK, r=8, o=PASSES)
+        k_codes = sb.tile([P, PACK, PASSES, P], U16, name="k_codes", align_bytes=64)
+        for u in range(2):
+            pair = slice(2 * u, 2 * u + 2)
+            nc.vector.tensor_copy(k_codes[:, pair].rearrange("p e o (j r) -> p e o j r", r=8), halves[:, pair])
+
+        kb_picked = sb.tile([P, PACK, P], F32, name="kb_picked", tag="words_then_kb")
+        pick(kb_picked, kb_pool)
         kb_turned = ps.tile([P, PACK, P], F32, name="kb_turned")
         for t in range(PACK):
             nc.tensor.transpose(kb_turned[:, t, :], kb_picked[:, t, :], ident[:])
-        kb_col = sb.tile([P, PACK], F32, name="kb_col")
+        kb_col = reuse.tile([P, PACK], F32, name="kb_col", offset=4 * N)
         nc.scalar.copy(kb_col[:], kb_turned[:, :, KB_ROW])
-
-        words = sb.tile([P, N], U32, name="words", tag="words_then_v")
-        nc.vector.tensor_copy(words[:], word_pool[:].bitcast(U32).indirect(offsets[:]))
 
         q_codes = sb.tile([P, PASSES * NQ], U32, name="q_codes", tag="kb_then_q", align_bytes=64)
         q_scale = sb.tile([P, PASSES * NQ], U8, name="q_scale", align_bytes=64)
         nc.vector.quantize_mx(out=q_codes[:].bitcast(FP8X4), scales=q_scale[:], in_=q_bf[:].rearrange("p o n t -> p (o n t)"))
 
-        halves = words[:].bitcast(U16).rearrange("p (j t r o) -> p t o j r", t=PACK, r=8, o=PASSES)
         p_all = sb.tile([P, PACK, NQ], F32, name="p_all")
-        k_codes = sb.tile([P, PACK, PASSES, P], U16, name="k_codes", align_bytes=64)
-        for u in range(2):
-            pair = slice(2 * u, 2 * u + 2)
-            nc.vector.tensor_copy(k_codes[:, pair].rearrange("p e o (j r) -> p e o j r", r=8), halves[:, pair])
-            for e in range(2):
-                t = 2 * u + e
-                acc = ps.tile([P, NQ], F32, name="scores%d" % t, tag="bank%d" % t)
-                for o in range(PASSES):
-                    nc.tensor.matmul_mx(
-                        out=acc[:],
-                        lhsT=k_codes[:, t, o, :].bitcast(FP4X4),
-                        lhsT_scale=planes[:, o, t * P : (t + 1) * P],
-                        rhs=q_codes[:, o * NQ : (o + 1) * NQ].bitcast(FP8X4),
-                        rhs_scale=q_scale[:, o * NQ : (o + 1) * NQ],
-                        start=(o == 0),
-                        stop=(o == PASSES - 1),
-                    )
-                nc.scalar.activation(p_all[:, t, :], acc[:], ACT.Silu, bias=kb_col[:, t : t + 1])
+        for t in range(PACK):
+            acc = ps.tile([P, NQ], F32, name="scores%d" % t, tag="bank%d" % t)
+            for o in range(PASSES):
+                nc.tensor.matmul_mx(
+                    out=acc[:],
+                    lhsT=k_codes[:, t, o, :].bitcast(FP4X4),
+                    lhsT_scale=planes[:, o, t * P : (t + 1) * P],
+                    rhs=q_codes[:, o * NQ : (o + 1) * NQ].bitcast(FP8X4),
+                    rhs_scale=q_scale[:, o * NQ : (o + 1) * NQ],
+                    start=(o == 0),
+                    stop=(o == PASSES - 1),
+                )
+            nc.scalar.activation(p_all[:, t, :], acc[:], ACT.Silu, bias=kb_col[:, t : t + 1])
 
-        vs_picked = pick(vs_pool, "vs_picked", "words_then_vs")
-        vs_turned = ps.tile([P, PACK, P], F32, name="vs_turned")
+        vs_picked = reuse.tile([P, PACK, P], F32, name="vs_picked", offset=0)
+        pick(vs_picked, vs_pool)
+        vs_turned = ps.tile([P, PACK, P], F32, name="vs_turned", tag="bank1")
         for t in range(PACK):
             nc.tensor.transpose(vs_turned[:, t, :], vs_picked[:, t, :], ident[:])
-        vs_col = sb.tile([P, PACK], F32, name="vs_col")
-        nc.scalar.copy(vs_col[:], vs_turned[:, :, 0])
 
-        v_picked = sb.tile([P, 2, P, 2], BF16, name="v_picked", tag="words_then_v")
+        v_picked = sb.tile([P, 2, P, 2], BF16, name="v_picked", tag="runs_then_q", align_bytes=64)
         nc.vector.tensor_copy(v_picked[:].rearrange("p u (j r) e -> p j u e r", r=8), v_pool[:].indirect(offsets[:]))
-        v_turned = ps.tile([P, 2, DV], F32, name="v_turned")
+        v_turned = ps.tile([P, 2, DV], F32, name="v_turned", tag="bank3")
         for u in range(2):
             nc.tensor.transpose(v_turned[:, u, :], v_picked[:, u].rearrange("p m e -> p (m e)").bitcast(F32), ident[:])
         v_bf = sb.tile([P, DV * PACK], BF16, name="v_bf", align_bytes=64)
@@ -155,7 +153,7 @@ def tile_attend_silu_kb_topkq128n512t2048_kernel(tc, qT, k_words, k_scales, vT, 
         nc.vector.tensor_tensor(
             w_bf[:].rearrange("p (c i) t -> p c t i", i=4),
             p_all[:].rearrange("p t (c i) -> p c t i", i=4),
-            vs_col[:].unsqueeze(1).unsqueeze(3).to_broadcast([P, NQ // 4, PACK, 4]),
+            vs_turned[:, :, 0:1].unsqueeze(1).to_broadcast([P, NQ // 4, PACK, 4]),
             MULT,
         )
 

@@ -39,17 +39,17 @@ def tile_attend_silu_kb_topkq128n512t2048_kernel(tc, qT, k_words, k_scales, vT, 
 
         offsets = sb.tile([P, N // 16], U16, name="offsets")
         nc.sync.dma_start(offsets[:], offs)
-        scale_pool = sb.tile([P, T], U8, name="scale_pool")
+        scale_pool = sb.tile([P, T], U8, name="scale_pool", tag="scales_then_v")
         nc.sync.dma_start(scale_pool[SCALE_ROW:, :].bitcast(I32), k_scales.rearrange("o f t -> f o t").bitcast(I32))
         vs_runs = sb.tile([P, RUN], F32, name="vs_runs", tag="runs_then_q", align_bytes=64)
         nc.sync.dma_start(vs_runs[:], vs[0].rearrange("(p j) -> p j", j=RUN))
 
-        word_pool = sb.tile([P, T], I32, name="word_pool", tag="words_then_kb")
+        word_pool = sb.tile([P, T], I32, name="word_pool")
         nc.sync.dma_start(word_pool[:], k_words[0].rearrange("p t b -> p (t b)").bitcast(I32))
         q_raw = reuse.tile([P, PASSES, PACK, NQ], F32, name="q_raw", offset=0)
         nc.sync.dma_start(q_raw[:], qT[0].rearrange("(o p t) n -> p o t n", o=PASSES, t=PACK))
 
-        kb_pool = sb.tile([P, T], F32, name="kb_pool", tag="kb_then_q", align_bytes=64)
+        kb_pool = sb.tile([P, T], F32, name="kb_pool")
         planes = sb.tile([P, PASSES, N], U8, name="planes", align_bytes=64)
         nc.vector.memset(kb_pool[:].bitcast(I32), 0)
         nc.scalar.dma_start(kb_pool[KB_ROW : KB_ROW + 1, :], kb[0:1, :])
@@ -63,20 +63,21 @@ def tile_attend_silu_kb_topkq128n512t2048_kernel(tc, qT, k_words, k_scales, vT, 
         warm_out = sb.tile([P, 1], F32, name="warm_out", tag="warm_then_vs")
         nc.scalar.activation(warm_out[:], warm_in[:], ACT.Silu)
 
-        scale_picked = sb.tile([P, N], U8, name="scale_picked", tag="scales_then_v", align_bytes=64)
+        scale_picked = sb.tile([P, N], U8, name="scale_picked")
         nc.vector.tensor_copy(scale_picked[:], scale_pool[:].indirect(offsets[:]))
         scale_sorted = sb.tile([P, N], U8, name="scale_sorted", align_bytes=64)
         nc.vector.tensor_copy(
             scale_sorted[:].bitcast(I32).rearrange("p (t j c) -> p t j c", t=PACK, c=2),
             scale_picked[:].bitcast(I32).rearrange("p (j t c) -> p t j c", t=PACK, c=2),
         )
+        v_pool = sb.tile([P, T], F32, name="v_pool", tag="scales_then_v")
+        nc.sync.dma_start(v_pool[:, : T // 2], vT[:, : T // 2])
         for quad in range(4):
             nc.sync.dma_start(
                 planes[32 * quad : 32 * quad + 4].bitcast(I32),
                 scale_sorted[SCALE_ROW + 8 * quad : SCALE_ROW + 8 * quad + 8, :].bitcast(I32),
             )
-        v_pool = sb.tile([P, T], F32, name="v_pool", tag="scales_then_v", align_bytes=64)
-        nc.sync.dma_start(v_pool[:], vT)
+        nc.sync.dma_start(v_pool[:, T // 2 :], vT[:, T // 2 :])
 
         vs_pool = sb.tile([P, T], F32, name="vs_pool", tag="warm_then_vs")
         for b in range(RUN // 4):
@@ -102,13 +103,7 @@ def tile_attend_silu_kb_topkq128n512t2048_kernel(tc, qT, k_words, k_scales, vT, 
         words = sb.tile([P, N], U32, name="words")
         nc.vector.tensor_copy(words[:], word_pool[:].bitcast(U32).indirect(offsets[:]))
 
-        halves = words[:].bitcast(U16).rearrange("p (j t r o) -> p t o j r", t=PACK, r=8, o=PASSES)
-        k_codes = sb.tile([P, PACK, PASSES, P], U16, name="k_codes", align_bytes=64)
-        for u in range(2):
-            pair = slice(2 * u, 2 * u + 2)
-            nc.vector.tensor_copy(k_codes[:, pair].rearrange("p e o (j r) -> p e o j r", r=8), halves[:, pair])
-
-        kb_picked = sb.tile([P, PACK, P], F32, name="kb_picked", tag="words_then_kb")
+        kb_picked = sb.tile([P, PACK, P], F32, name="kb_picked")
         pick(kb_picked, kb_pool)
         kb_turned = ps.tile([P, PACK, P], F32, name="kb_turned")
         for t in range(PACK):
@@ -116,7 +111,13 @@ def tile_attend_silu_kb_topkq128n512t2048_kernel(tc, qT, k_words, k_scales, vT, 
         kb_col = reuse.tile([P, PACK], F32, name="kb_col", offset=4 * N)
         nc.scalar.copy(kb_col[:], kb_turned[:, :, KB_ROW])
 
-        q_codes = sb.tile([P, PASSES * NQ], U32, name="q_codes", tag="kb_then_q", align_bytes=64)
+        halves = words[:].bitcast(U16).rearrange("p (j t r o) -> p t o j r", t=PACK, r=8, o=PASSES)
+        k_codes = sb.tile([P, PACK, PASSES, P], U16, name="k_codes", align_bytes=64)
+        for u in range(2):
+            pair = slice(2 * u, 2 * u + 2)
+            nc.vector.tensor_copy(k_codes[:, pair].rearrange("p e o (j r) -> p e o j r", r=8), halves[:, pair])
+
+        q_codes = sb.tile([P, PASSES * NQ], U32, name="q_codes", align_bytes=64)
         q_scale = sb.tile([P, PASSES * NQ], U8, name="q_scale", align_bytes=64)
         nc.vector.quantize_mx(out=q_codes[:].bitcast(FP8X4), scales=q_scale[:], in_=q_bf[:].rearrange("p o n t -> p (o n t)"))
 
@@ -175,5 +176,5 @@ def tile_attend_silu_kb_topkq128n512t2048_kernel(tc, qT, k_words, k_scales, vT, 
             stop=True,
         )
         y = sb.tile([NQ, DV], F32, name="y")
-        nc.vector.tensor_scalar(y[:], y_acc[:], 1.0 / 16.0, None, MULT)
-        nc.sync.dma_start(out[0], y[:])
+        nc.scalar.activation(y[:], y_acc[:], ACT.Copy, scale=1.0 / 16.0)
+        nc.scalar.dma_start(out[0], y[:])

@@ -21,9 +21,10 @@ MULT = mybir.AluOpType.mult
 P = 128
 PACK = 4
 PASSES = D // (P * PACK)
-KB_ROW = 8
+KB_ROW = 127
 SCALE_ROW = 96
 RUN = T // P
+V_EARLY = 3 * T // 4
 
 
 def slot_order(ap):
@@ -38,23 +39,23 @@ def tile_attend_silu_kb_topkq128n512t2048_kernel(tc, qT, k_words, k_scales, vT, 
         ps = ctx.enter_context(tc.psum_pool(name="ps", bufs=1))
 
         offsets = sb.tile([P, N // 16], U16, name="offsets")
-        nc.sync.dma_start(offsets[:], offs)
-        scale_pool = sb.tile([P, T], U8, name="scale_pool", tag="scales_then_v")
+        kb_pool = sb.tile([P, T], F32, name="kb_pool")
+        nc.sync.dma_start(kb_pool[KB_ROW:, :], kb[0:1, :])
+        scale_pool = sb.tile([P, T], U8, name="scale_pool")
         nc.sync.dma_start(scale_pool[SCALE_ROW:, :].bitcast(I32), k_scales.rearrange("o f t -> f o t").bitcast(I32))
+        nc.sync.dma_start(offsets[:], offs)
         vs_runs = sb.tile([P, RUN], F32, name="vs_runs", tag="runs_then_q", align_bytes=64)
-        nc.sync.dma_start(vs_runs[:], vs[0].rearrange("(p j) -> p j", j=RUN))
+        nc.scalar.dma_start(vs_runs[:], vs[0].rearrange("(p j) -> p j", j=RUN))
 
         word_pool = sb.tile([P, T], I32, name="word_pool")
         nc.sync.dma_start(word_pool[:], k_words[0].rearrange("p t b -> p (t b)").bitcast(I32))
         q_raw = reuse.tile([P, PASSES, PACK, NQ], F32, name="q_raw", offset=0)
         nc.sync.dma_start(q_raw[:], qT[0].rearrange("(o p t) n -> p o t n", o=PASSES, t=PACK))
 
-        kb_pool = sb.tile([P, T], F32, name="kb_pool")
         planes = sb.tile([P, PASSES, N], U8, name="planes", align_bytes=64)
-        nc.vector.memset(kb_pool[:].bitcast(I32), 0)
-        nc.scalar.dma_start(kb_pool[KB_ROW : KB_ROW + 1, :], kb[0:1, :])
         nc.vector.memset(scale_pool[:SCALE_ROW, :].bitcast(I32), 0)
-        nc.vector.memset(planes[:].bitcast(I32), 0)
+        nc.vector.memset(kb_pool[:KB_ROW, :].bitcast(I32), 0)
+        nc.gpsimd.memset(planes[:].bitcast(I32), 0)
 
         warm_in = sb.tile([P, 1], F32, name="warm_in")
         nc.gpsimd.memset(warm_in[:], 0.0)
@@ -63,21 +64,26 @@ def tile_attend_silu_kb_topkq128n512t2048_kernel(tc, qT, k_words, k_scales, vT, 
         warm_out = sb.tile([P, 1], F32, name="warm_out", tag="warm_then_vs")
         nc.scalar.activation(warm_out[:], warm_in[:], ACT.Silu)
 
+        def pick(picked, pool):
+            nc.vector.tensor_copy(slot_order(picked[:].bitcast(U32)), pool[:].bitcast(U32).indirect(offsets[:]))
+
         scale_picked = sb.tile([P, N], U8, name="scale_picked")
         nc.vector.tensor_copy(scale_picked[:], scale_pool[:].indirect(offsets[:]))
+        kb_picked = sb.tile([P, PACK, P], F32, name="kb_picked")
+        pick(kb_picked, kb_pool)
         scale_sorted = sb.tile([P, N], U8, name="scale_sorted", align_bytes=64)
         nc.vector.tensor_copy(
             scale_sorted[:].bitcast(I32).rearrange("p (t j c) -> p t j c", t=PACK, c=2),
             scale_picked[:].bitcast(I32).rearrange("p (j t c) -> p t j c", t=PACK, c=2),
         )
-        v_pool = sb.tile([P, T], F32, name="v_pool", tag="scales_then_v")
-        nc.sync.dma_start(v_pool[:, : T // 2], vT[:, : T // 2])
+        v_pool = sb.tile([P, T], F32, name="v_pool")
+        nc.sync.dma_start(v_pool[:, :V_EARLY], vT[:, :V_EARLY])
         for quad in range(4):
             nc.sync.dma_start(
                 planes[32 * quad : 32 * quad + 4].bitcast(I32),
                 scale_sorted[SCALE_ROW + 8 * quad : SCALE_ROW + 8 * quad + 8, :].bitcast(I32),
             )
-        nc.sync.dma_start(v_pool[:, T // 2 :], vT[:, T // 2 :])
+        nc.sync.dma_start(v_pool[:, V_EARLY:], vT[:, V_EARLY:])
 
         vs_pool = sb.tile([P, T], F32, name="vs_pool", tag="warm_then_vs")
         for b in range(RUN // 4):
@@ -97,25 +103,22 @@ def tile_attend_silu_kb_topkq128n512t2048_kernel(tc, qT, k_words, k_scales, vT, 
                 ACT.Copy,
             )
 
-        def pick(picked, pool):
-            nc.vector.tensor_copy(slot_order(picked[:].bitcast(U32)), pool[:].bitcast(U32).indirect(offsets[:]))
+        words = [sb.tile([P, N // 2], U32, name="words%d" % h) for h in range(2)]
+        for h in range(2):
+            nc.vector.tensor_copy(words[h][:], word_pool[:].bitcast(U32).indirect(offsets[:, 16 * h : 16 * h + 16]))
 
-        words = sb.tile([P, N], U32, name="words")
-        nc.vector.tensor_copy(words[:], word_pool[:].bitcast(U32).indirect(offsets[:]))
-
-        kb_picked = sb.tile([P, PACK, P], F32, name="kb_picked")
-        pick(kb_picked, kb_pool)
         kb_turned = ps.tile([P, PACK, P], F32, name="kb_turned")
         for t in range(PACK):
             nc.tensor.transpose(kb_turned[:, t, :], kb_picked[:, t, :], ident[:])
         kb_col = reuse.tile([P, PACK], F32, name="kb_col", offset=4 * N)
         nc.scalar.copy(kb_col[:], kb_turned[:, :, KB_ROW])
 
-        halves = words[:].bitcast(U16).rearrange("p (j t r o) -> p t o j r", t=PACK, r=8, o=PASSES)
         k_codes = sb.tile([P, PACK, PASSES, P], U16, name="k_codes", align_bytes=64)
-        for u in range(2):
-            pair = slice(2 * u, 2 * u + 2)
-            nc.vector.tensor_copy(k_codes[:, pair].rearrange("p e o (j r) -> p e o j r", r=8), halves[:, pair])
+        for h in range(2):
+            nc.vector.tensor_copy(
+                k_codes[:, :, :, 64 * h : 64 * h + 64].rearrange("p t o (j r) -> p t o j r", r=8),
+                words[h][:].bitcast(U16).rearrange("p (j t r o) -> p t o j r", t=PACK, r=8, o=PASSES),
+            )
 
         q_codes = sb.tile([P, PASSES * NQ], U32, name="q_codes", align_bytes=64)
         q_scale = sb.tile([P, PASSES * NQ], U8, name="q_scale", align_bytes=64)

@@ -24,7 +24,7 @@ PASSES = D // (P * PACK)
 KB_ROW = 127
 SCALE_ROW = 96
 RUN = T // P
-V_EARLY = 3 * T // 4
+V_EARLY = 5 * T // 8
 
 
 def slot_order(ap):
@@ -39,44 +39,48 @@ def tile_attend_silu_kb_topkq128n512t2048_kernel(tc, qT, k_words, k_scales, vT, 
         ps = ctx.enter_context(tc.psum_pool(name="ps", bufs=1))
 
         offsets = sb.tile([P, N // 16], U16, name="offsets")
-        kb_pool = sb.tile([P, T], F32, name="kb_pool")
-        nc.sync.dma_start(kb_pool[KB_ROW:, :], kb[0:1, :])
-        scale_pool = sb.tile([P, T], U8, name="scale_pool")
-        nc.sync.dma_start(scale_pool[SCALE_ROW:, :].bitcast(I32), k_scales.rearrange("o f t -> f o t").bitcast(I32))
         nc.sync.dma_start(offsets[:], offs)
+        scale_pool = sb.tile([P, T], U8, name="scale_pool", tag="scales_then_v")
+        nc.sync.dma_start(scale_pool[SCALE_ROW:, :].bitcast(I32), k_scales.rearrange("o f t -> f o t").bitcast(I32))
+        kb_pool = sb.tile([P, T], F32, name="kb_pool")
         vs_runs = sb.tile([P, RUN], F32, name="vs_runs", tag="runs_then_q", align_bytes=64)
         nc.scalar.dma_start(vs_runs[:], vs[0].rearrange("(p j) -> p j", j=RUN))
+        nc.scalar.dma_start(kb_pool[KB_ROW:, :], kb[0:1, :])
 
         word_pool = sb.tile([P, T], I32, name="word_pool")
         nc.sync.dma_start(word_pool[:], k_words[0].rearrange("p t b -> p (t b)").bitcast(I32))
         q_raw = reuse.tile([P, PASSES, PACK, NQ], F32, name="q_raw", offset=0)
-        nc.sync.dma_start(q_raw[:], qT[0].rearrange("(o p t) n -> p o t n", o=PASSES, t=PACK))
+        for o in range(PASSES):
+            nc.sync.dma_start(q_raw[:, o], qT[0].rearrange("(o p t) n -> p o t n", o=PASSES, t=PACK)[:, o])
 
         planes = sb.tile([P, PASSES, N], U8, name="planes", align_bytes=64)
         nc.vector.memset(scale_pool[:SCALE_ROW, :].bitcast(I32), 0)
-        nc.vector.memset(kb_pool[:KB_ROW, :].bitcast(I32), 0)
-        nc.gpsimd.memset(planes[:].bitcast(I32), 0)
 
         warm_in = sb.tile([P, 1], F32, name="warm_in")
         nc.gpsimd.memset(warm_in[:], 0.0)
         ident = sb.tile([P, P], F32, name="ident")
         make_identity(nc, ident[:])
+        nc.vector.memset(kb_pool[:KB_ROW, :].bitcast(I32), 0)
+        nc.gpsimd.memset(planes[:].bitcast(I32), 0)
         warm_out = sb.tile([P, 1], F32, name="warm_out", tag="warm_then_vs")
         nc.scalar.activation(warm_out[:], warm_in[:], ACT.Silu)
 
-        def pick(picked, pool):
-            nc.vector.tensor_copy(slot_order(picked[:].bitcast(U32)), pool[:].bitcast(U32).indirect(offsets[:]))
+        def pick(picked, pool, first, last):
+            nc.vector.tensor_copy(
+                slot_order(picked[:].bitcast(U32))[:, first:last],
+                pool[:].bitcast(U32).indirect(offsets[:, 2 * first : 2 * last]),
+            )
 
         scale_picked = sb.tile([P, N], U8, name="scale_picked")
         nc.vector.tensor_copy(scale_picked[:], scale_pool[:].indirect(offsets[:]))
-        kb_picked = sb.tile([P, PACK, P], F32, name="kb_picked")
-        pick(kb_picked, kb_pool)
         scale_sorted = sb.tile([P, N], U8, name="scale_sorted", align_bytes=64)
         nc.vector.tensor_copy(
             scale_sorted[:].bitcast(I32).rearrange("p (t j c) -> p t j c", t=PACK, c=2),
             scale_picked[:].bitcast(I32).rearrange("p (j t c) -> p t j c", t=PACK, c=2),
         )
-        v_pool = sb.tile([P, T], F32, name="v_pool")
+        kb_picked = sb.tile([P, PACK, P], F32, name="kb_picked")
+        pick(kb_picked, kb_pool, 0, 16)
+        v_pool = sb.tile([P, T], F32, name="v_pool", tag="scales_then_v")
         nc.sync.dma_start(v_pool[:, :V_EARLY], vT[:, :V_EARLY])
         for quad in range(4):
             nc.sync.dma_start(
@@ -140,7 +144,7 @@ def tile_attend_silu_kb_topkq128n512t2048_kernel(tc, qT, k_words, k_scales, vT, 
             nc.scalar.activation(p_all[:, t, :], acc[:], ACT.Silu, bias=kb_col[:, t : t + 1])
 
         vs_picked = reuse.tile([P, PACK, P], F32, name="vs_picked", offset=0)
-        pick(vs_picked, vs_pool)
+        pick(vs_picked, vs_pool, 0, 16)
         vs_turned = ps.tile([P, PACK, P], F32, name="vs_turned", tag="bank1")
         for t in range(PACK):
             nc.tensor.transpose(vs_turned[:, t, :], vs_picked[:, t, :], ident[:])

@@ -23,8 +23,8 @@ PACK = 4
 PASSES = D // (P * PACK)
 KB_ROW = 127
 SCALE_ROW = 96
-RUN = T // P
-V_EARLY = 5 * T // 8
+VS_HEAD = 3 * T // 4
+V_EARLY = 3 * T // 4
 
 
 def slot_order(ap):
@@ -43,8 +43,7 @@ def tile_attend_silu_kb_topkq128n512t2048_kernel(tc, qT, k_words, k_scales, vT, 
         scale_pool = sb.tile([P, T], U8, name="scale_pool", tag="scales_then_v")
         nc.sync.dma_start(scale_pool[SCALE_ROW:, :].bitcast(I32), k_scales.rearrange("o f t -> f o t").bitcast(I32))
         kb_pool = sb.tile([P, T], F32, name="kb_pool")
-        vs_runs = sb.tile([P, RUN], F32, name="vs_runs", tag="runs_then_q", align_bytes=64)
-        nc.scalar.dma_start(vs_runs[:], vs[0].rearrange("(p j) -> p j", j=RUN))
+        vs_pool = sb.tile([P, T], F32, name="vs_pool")
         nc.scalar.dma_start(kb_pool[KB_ROW:, :], kb[0:1, :])
 
         word_pool = sb.tile([P, T], I32, name="word_pool")
@@ -52,17 +51,17 @@ def tile_attend_silu_kb_topkq128n512t2048_kernel(tc, qT, k_words, k_scales, vT, 
         q_raw = reuse.tile([P, PASSES, PACK, NQ], F32, name="q_raw", offset=0)
         for o in range(PASSES):
             nc.sync.dma_start(q_raw[:, o], qT[0].rearrange("(o p t) n -> p o t n", o=PASSES, t=PACK)[:, o])
+        nc.sync.dma_start(vs_pool[KB_ROW:, :], vs[0:1, :])
 
         planes = sb.tile([P, PASSES, N], U8, name="planes", align_bytes=64)
         nc.vector.memset(scale_pool[:SCALE_ROW, :].bitcast(I32), 0)
 
-        warm_in = sb.tile([P, 1], F32, name="warm_in")
+        warm_in = sb.tile([P, 1], F32, name="warm_in", tag="warm_then_ident")
         nc.gpsimd.memset(warm_in[:], 0.0)
-        ident = sb.tile([P, P], F32, name="ident")
-        make_identity(nc, ident[:])
         nc.vector.memset(kb_pool[:KB_ROW, :].bitcast(I32), 0)
-        nc.gpsimd.memset(planes[:].bitcast(I32), 0)
-        warm_out = sb.tile([P, 1], F32, name="warm_out", tag="warm_then_vs")
+        nc.vector.memset(planes[:].bitcast(I32), 0)
+        nc.vector.memset(vs_pool[:KB_ROW, :VS_HEAD].bitcast(I32), 0)
+        warm_out = sb.tile([P, 1], F32, name="warm_out", tag="runs_then_q", align_bytes=64)
         nc.scalar.activation(warm_out[:], warm_in[:], ACT.Silu)
 
         def pick(picked, pool, first, last):
@@ -73,31 +72,25 @@ def tile_attend_silu_kb_topkq128n512t2048_kernel(tc, qT, k_words, k_scales, vT, 
 
         scale_picked = sb.tile([P, N], U8, name="scale_picked")
         nc.vector.tensor_copy(scale_picked[:], scale_pool[:].indirect(offsets[:]))
+        nc.vector.memset(vs_pool[:KB_ROW, VS_HEAD:].bitcast(I32), 0)
         scale_sorted = sb.tile([P, N], U8, name="scale_sorted", align_bytes=64)
         nc.vector.tensor_copy(
             scale_sorted[:].bitcast(I32).rearrange("p (t j c) -> p t j c", t=PACK, c=2),
             scale_picked[:].bitcast(I32).rearrange("p (j t c) -> p t j c", t=PACK, c=2),
         )
+        ident = sb.tile([P, P], F32, name="ident", tag="warm_then_ident")
+        make_identity(nc, ident[:])
         kb_picked = sb.tile([P, PACK, P], F32, name="kb_picked")
         pick(kb_picked, kb_pool, 0, 16)
         v_pool = sb.tile([P, T], F32, name="v_pool", tag="scales_then_v")
-        nc.sync.dma_start(v_pool[:, :V_EARLY], vT[:, :V_EARLY])
+        nc.sync.dma_start(v_pool[:, : V_EARLY // 2], vT[:, : V_EARLY // 2])
+        nc.sync.dma_start(v_pool[:, V_EARLY // 2 : V_EARLY], vT[:, V_EARLY // 2 : V_EARLY])
         for quad in range(4):
             nc.sync.dma_start(
                 planes[32 * quad : 32 * quad + 4].bitcast(I32),
                 scale_sorted[SCALE_ROW + 8 * quad : SCALE_ROW + 8 * quad + 8, :].bitcast(I32),
             )
         nc.sync.dma_start(v_pool[:, V_EARLY:], vT[:, V_EARLY:])
-
-        vs_pool = sb.tile([P, T], F32, name="vs_pool", tag="warm_then_vs")
-        for b in range(RUN // 4):
-            spread = ps.tile([P, 4, P], F32, name="spread%d" % b, tag="bank%d" % b)
-            for j in range(4):
-                nc.tensor.transpose(spread[:, j, :], vs_runs[:, 4 * b + j : 4 * b + j + 1].to_broadcast([P, P]), ident[:])
-            nc.scalar.copy(
-                vs_pool[:].rearrange("p (m b j) -> p b m j", b=RUN // 4, j=4)[:, b],
-                spread[:].rearrange("p j m -> p m j"),
-            )
 
         q_bf = sb.tile([P, PASSES, NQ, PACK], BF16, name="q_bf", tag="runs_then_q", align_bytes=64)
         for o in range(PASSES):
@@ -161,7 +154,7 @@ def tile_attend_silu_kb_topkq128n512t2048_kernel(tc, qT, k_words, k_scales, vT, 
         nc.vector.tensor_tensor(
             w_bf[:].rearrange("p (c i) t -> p c t i", i=4),
             p_all[:].rearrange("p t (c i) -> p c t i", i=4),
-            vs_turned[:, :, 0:1].unsqueeze(1).to_broadcast([P, NQ // 4, PACK, 4]),
+            vs_turned[:, :, KB_ROW:].unsqueeze(1).to_broadcast([P, NQ // 4, PACK, 4]),
             MULT,
         )
 

@@ -23,8 +23,8 @@ PACK = 4
 PASSES = D // (P * PACK)
 KB_ROW = 127
 SCALE_ROW = 96
-VS_HEAD = 3 * T // 4
-V_EARLY = 3 * T // 4
+VS_HEAD = 64
+V_EARLY = T // 4
 
 
 def slot_order(ap):
@@ -53,14 +53,18 @@ def tile_attend_silu_kb_topkq128n512t2048_kernel(tc, qT, k_words, k_scales, vT, 
             nc.sync.dma_start(q_raw[:, o], qT[0].rearrange("(o p t) n -> p o t n", o=PASSES, t=PACK)[:, o])
         nc.sync.dma_start(vs_pool[KB_ROW:, :], vs[0:1, :])
 
-        planes = sb.tile([P, PASSES, N], U8, name="planes", align_bytes=64)
+        moved = sb.tile([P, PASSES, N], U8, name="moved", align_bytes=64)
         nc.vector.memset(scale_pool[:SCALE_ROW, :].bitcast(I32), 0)
 
-        warm_in = sb.tile([P, 1], F32, name="warm_in", tag="warm_then_ident")
+        warm_in = sb.tile([P, 1], F32, name="warm_in")
         nc.gpsimd.memset(warm_in[:], 0.0)
         nc.vector.memset(kb_pool[:KB_ROW, :].bitcast(I32), 0)
-        nc.vector.memset(planes[:].bitcast(I32), 0)
+        nc.vector.memset(moved[:].bitcast(I32), 0)
+        ident = sb.tile([P, P], F32, name="ident")
+        nc.vector.memset(ident[:], 0.0)
+        make_identity(nc, ident[:], nomemset=True)
         nc.vector.memset(vs_pool[:KB_ROW, :VS_HEAD].bitcast(I32), 0)
+        nc.gpsimd.memset(vs_pool[:KB_ROW, VS_HEAD - 8 :].bitcast(I32), 0)
         warm_out = sb.tile([P, 1], F32, name="warm_out", tag="runs_then_q", align_bytes=64)
         nc.scalar.activation(warm_out[:], warm_in[:], ACT.Silu)
 
@@ -70,25 +74,16 @@ def tile_attend_silu_kb_topkq128n512t2048_kernel(tc, qT, k_words, k_scales, vT, 
                 pool[:].bitcast(U32).indirect(offsets[:, 2 * first : 2 * last]),
             )
 
-        scale_picked = sb.tile([P, N], U8, name="scale_picked")
+        scale_picked = sb.tile([P, N], U8, name="scale_picked", tag="scales_then_vs")
         nc.vector.tensor_copy(scale_picked[:], scale_pool[:].indirect(offsets[:]))
-        nc.vector.memset(vs_pool[:KB_ROW, VS_HEAD:].bitcast(I32), 0)
-        scale_sorted = sb.tile([P, N], U8, name="scale_sorted", align_bytes=64)
-        nc.vector.tensor_copy(
-            scale_sorted[:].bitcast(I32).rearrange("p (t j c) -> p t j c", t=PACK, c=2),
-            scale_picked[:].bitcast(I32).rearrange("p (j t c) -> p t j c", t=PACK, c=2),
-        )
-        ident = sb.tile([P, P], F32, name="ident", tag="warm_then_ident")
-        make_identity(nc, ident[:])
         kb_picked = sb.tile([P, PACK, P], F32, name="kb_picked")
         pick(kb_picked, kb_pool, 0, 16)
         v_pool = sb.tile([P, T], F32, name="v_pool", tag="scales_then_v")
-        nc.sync.dma_start(v_pool[:, : V_EARLY // 2], vT[:, : V_EARLY // 2])
-        nc.sync.dma_start(v_pool[:, V_EARLY // 2 : V_EARLY], vT[:, V_EARLY // 2 : V_EARLY])
+        nc.sync.dma_start(v_pool[:, :V_EARLY], vT[:, :V_EARLY])
         for quad in range(4):
             nc.sync.dma_start(
-                planes[32 * quad : 32 * quad + 4].bitcast(I32),
-                scale_sorted[SCALE_ROW + 8 * quad : SCALE_ROW + 8 * quad + 8, :].bitcast(I32),
+                moved[32 * quad : 32 * quad + 4].bitcast(I32),
+                scale_picked[SCALE_ROW + 8 * quad : SCALE_ROW + 8 * quad + 8, :].bitcast(I32),
             )
         nc.sync.dma_start(v_pool[:, V_EARLY:], vT[:, V_EARLY:])
 
@@ -121,6 +116,12 @@ def tile_attend_silu_kb_topkq128n512t2048_kernel(tc, qT, k_words, k_scales, vT, 
         q_scale = sb.tile([P, PASSES * NQ], U8, name="q_scale", align_bytes=64)
         nc.vector.quantize_mx(out=q_codes[:].bitcast(FP8X4), scales=q_scale[:], in_=q_bf[:].rearrange("p o n t -> p (o n t)"))
 
+        planes = sb.tile([P, PASSES, N], U8, name="planes", align_bytes=64)
+        nc.vector.tensor_copy(
+            planes[:].bitcast(I32).rearrange("p o (t j c) -> p o t j c", t=PACK, c=2),
+            moved[:].bitcast(I32).rearrange("p o (j t c) -> p o t j c", t=PACK, c=2),
+        )
+
         p_all = sb.tile([P, PACK, NQ], F32, name="p_all")
         for t in range(PACK):
             acc = ps.tile([P, NQ], F32, name="scores%d" % t, tag="bank%d" % t)
@@ -136,7 +137,7 @@ def tile_attend_silu_kb_topkq128n512t2048_kernel(tc, qT, k_words, k_scales, vT, 
                 )
             nc.scalar.activation(p_all[:, t, :], acc[:], ACT.Silu, bias=kb_col[:, t : t + 1])
 
-        vs_picked = reuse.tile([P, PACK, P], F32, name="vs_picked", offset=0)
+        vs_picked = sb.tile([P, PACK, P], F32, name="vs_picked", tag="scales_then_vs")
         pick(vs_picked, vs_pool, 0, 16)
         vs_turned = ps.tile([P, PACK, P], F32, name="vs_turned", tag="bank1")
         for t in range(PACK):
@@ -144,7 +145,7 @@ def tile_attend_silu_kb_topkq128n512t2048_kernel(tc, qT, k_words, k_scales, vT, 
 
         v_picked = sb.tile([P, 2, P, 2], BF16, name="v_picked", tag="runs_then_q", align_bytes=64)
         nc.vector.tensor_copy(v_picked[:].rearrange("p u (j r) e -> p j u e r", r=8), v_pool[:].indirect(offsets[:]))
-        v_turned = ps.tile([P, 2, DV], F32, name="v_turned", tag="bank3")
+        v_turned = ps.tile([P, 2, DV], F32, name="v_turned", tag="bank0")
         for u in range(2):
             nc.tensor.transpose(v_turned[:, u, :], v_picked[:, u].rearrange("p m e -> p (m e)").bitcast(F32), ident[:])
         v_bf = sb.tile([P, DV * PACK], BF16, name="v_bf", align_bytes=64)

@@ -22,7 +22,7 @@ P = 128
 PACK = 4
 PASSES = D // (P * PACK)
 KB_ROW = 127
-SCALE_ROW = 96
+SCALE_ROWS = 32
 VS_HEAD = 64
 V_EARLY = T // 4
 
@@ -41,25 +41,26 @@ def tile_attend_silu_kb_topkq128n512t2048_kernel(tc, qT, k_words, k_scales, vT, 
         offsets = sb.tile([P, N // 16], U16, name="offsets")
         nc.sync.dma_start(offsets[:], offs)
         scale_pool = sb.tile([P, T], U8, name="scale_pool", tag="scales_then_v")
-        nc.sync.dma_start(scale_pool[SCALE_ROW:, :].bitcast(I32), k_scales.rearrange("o f t -> f o t").bitcast(I32))
+        nc.sync.dma_start(scale_pool[:SCALE_ROWS, :].bitcast(I32), k_scales.rearrange("o f t -> f o t").bitcast(I32))
         kb_pool = sb.tile([P, T], F32, name="kb_pool")
         vs_pool = sb.tile([P, T], F32, name="vs_pool")
         nc.scalar.dma_start(kb_pool[KB_ROW:, :], kb[0:1, :])
+        nc.scalar.dma_start(vs_pool[KB_ROW:, :], vs[0:1, :])
 
         word_pool = sb.tile([P, T], I32, name="word_pool")
         nc.sync.dma_start(word_pool[:], k_words[0].rearrange("p t b -> p (t b)").bitcast(I32))
         q_raw = reuse.tile([P, PASSES, PACK, NQ], F32, name="q_raw", offset=0)
         for o in range(PASSES):
             nc.sync.dma_start(q_raw[:, o], qT[0].rearrange("(o p t) n -> p o t n", o=PASSES, t=PACK)[:, o])
-        nc.sync.dma_start(vs_pool[KB_ROW:, :], vs[0:1, :])
 
         moved = sb.tile([P, PASSES, N], U8, name="moved", align_bytes=64)
-        nc.vector.memset(scale_pool[:SCALE_ROW, :].bitcast(I32), 0)
+        nc.vector.memset(scale_pool[32:64, :].bitcast(I32), 0)
+        nc.vector.memset(scale_pool[64:, :].bitcast(I32), 0)
 
         warm_in = sb.tile([P, 1], F32, name="warm_in")
         nc.gpsimd.memset(warm_in[:], 0.0)
         nc.vector.memset(kb_pool[:KB_ROW, :].bitcast(I32), 0)
-        nc.vector.memset(moved[:].bitcast(I32), 0)
+        nc.gpsimd.memset(moved[:].bitcast(I32), 0)
         ident = sb.tile([P, P], F32, name="ident")
         nc.vector.memset(ident[:], 0.0)
         make_identity(nc, ident[:], nomemset=True)
@@ -83,7 +84,7 @@ def tile_attend_silu_kb_topkq128n512t2048_kernel(tc, qT, k_words, k_scales, vT, 
         for quad in range(4):
             nc.sync.dma_start(
                 moved[32 * quad : 32 * quad + 4].bitcast(I32),
-                scale_picked[SCALE_ROW + 8 * quad : SCALE_ROW + 8 * quad + 8, :].bitcast(I32),
+                scale_picked[8 * quad : 8 * quad + 8, :].bitcast(I32),
             )
         nc.sync.dma_start(v_pool[:, V_EARLY:], vT[:, V_EARLY:])
 

@@ -40,7 +40,7 @@ def tile_attend_silu_kb_topkq128n512t2048_kernel(tc, qT, k_words, k_scales, vT, 
 
         offsets = sb.tile([P, N // 16], U16, name="offsets")
         nc.sync.dma_start(offsets[:], offs)
-        scale_pool = sb.tile([P, T], U8, name="scale_pool", tag="scales_then_v")
+        scale_pool = sb.tile([P, T], U8, name="scale_pool")
         nc.sync.dma_start(scale_pool[:SCALE_ROWS, :].bitcast(I32), k_scales.rearrange("o f t -> f o t").bitcast(I32))
         kb_pool = sb.tile([P, T], F32, name="kb_pool")
         vs_pool = sb.tile([P, T], F32, name="vs_pool")
@@ -79,9 +79,9 @@ def tile_attend_silu_kb_topkq128n512t2048_kernel(tc, qT, k_words, k_scales, vT, 
         nc.vector.tensor_copy(scale_picked[:], scale_pool[:].indirect(offsets[:]))
         kb_picked = sb.tile([P, PACK, P], F32, name="kb_picked")
         pick(kb_picked, kb_pool, 0, 16)
-        v_pool = sb.tile([P, T], F32, name="v_pool", tag="scales_then_v")
+        v_pool = sb.tile([P, T], F32, name="v_pool")
         nc.sync.dma_start(v_pool[:, :V_EARLY], vT[:, :V_EARLY])
-        for quad in range(4):
+        for quad in (0, 2, 1, 3):
             nc.sync.dma_start(
                 moved[32 * quad : 32 * quad + 4].bitcast(I32),
                 scale_picked[8 * quad : 8 * quad + 8, :].bitcast(I32),
@@ -140,7 +140,7 @@ def tile_attend_silu_kb_topkq128n512t2048_kernel(tc, qT, k_words, k_scales, vT, 
 
         vs_picked = sb.tile([P, PACK, P], F32, name="vs_picked", tag="scales_then_vs")
         pick(vs_picked, vs_pool, 0, 16)
-        vs_turned = ps.tile([P, PACK, P], F32, name="vs_turned", tag="bank1")
+        vs_turned = ps.tile([P, PACK, P], F32, name="vs_turned")
         for t in range(PACK):
             nc.tensor.transpose(vs_turned[:, t, :], vs_picked[:, t, :], ident[:])
 

@@ -178,5 +178,5 @@ def tile_attend_silu_kb_topkq128n512t2048_kernel(tc, qT, k_words, k_scales, vT, 
             stop=True,
         )
         y = sb.tile([NQ, DV], F32, name="y")
-        nc.scalar.activation(y[:], y_acc[:], ACT.Copy, scale=1.0 / 16.0)
-        nc.scalar.dma_start(out[0], y[:])
+        nc.vector.tensor_scalar_mul(y[:], y_acc[:], 1.0 / 16.0)
+        nc.sync.dma_start(out[0], y[:])

@@ -24,7 +24,7 @@ PASSES = D // (P * PACK)
 KB_ROW = 127
 SCALE_ROWS = 32
 VS_HEAD = 64
-V_EARLY = T // 4
+V_EARLY = 3 * T // 8
 
 
 def slot_order(ap):

@@ -25,6 +25,7 @@ KB_ROW = 127
 SCALE_ROWS = 32
 VS_HEAD = 64
 V_EARLY = 3 * T // 8
+HALF = DV // 2
 
 
 def slot_order(ap):
@@ -66,7 +67,7 @@ def tile_attend_silu_kb_topkq128n512t2048_kernel(tc, qT, k_words, k_scales, vT, 
         make_identity(nc, ident[:], nomemset=True)
         nc.vector.memset(vs_pool[:KB_ROW, :VS_HEAD].bitcast(I32), 0)
         nc.gpsimd.memset(vs_pool[:KB_ROW, VS_HEAD - 8 :].bitcast(I32), 0)
-        warm_out = sb.tile([P, 1], F32, name="warm_out", tag="runs_then_q", align_bytes=64)
+        warm_out = sb.tile([P, 1], F32, name="warm_out")
         nc.scalar.activation(warm_out[:], warm_in[:], ACT.Silu)
 
         def pick(picked, pool, first, last):
@@ -150,7 +151,11 @@ def tile_attend_silu_kb_topkq128n512t2048_kernel(tc, qT, k_words, k_scales, vT, 
         for u in range(2):
             nc.tensor.transpose(v_turned[:, u, :], v_picked[:, u].rearrange("p m e -> p (m e)").bitcast(F32), ident[:])
         v_bf = sb.tile([P, DV * PACK], BF16, name="v_bf", align_bytes=64)
-        nc.scalar.copy(v_bf[:].bitcast(F32).rearrange("p (c u) -> p c u", u=2), v_turned[:].rearrange("p u c -> p c u"))
+        for h in range(2):
+            nc.scalar.copy(
+                v_bf[:].bitcast(F32).rearrange("p (c u) -> p c u", u=2)[:, h * HALF : (h + 1) * HALF],
+                v_turned[:].rearrange("p u c -> p c u")[:, h * HALF : (h + 1) * HALF],
+            )
 
         w_bf = sb.tile([P, NQ, PACK], BF16, name="w_bf", align_bytes=64)
         nc.vector.tensor_tensor(
@@ -165,18 +170,24 @@ def tile_attend_silu_kb_topkq128n512t2048_kernel(tc, qT, k_words, k_scales, vT, 
         nc.vector.quantize_mx(out=w_codes[:].bitcast(FP8X4), scales=w_scale[:], in_=w_bf[:].rearrange("p q t -> p (q t)"))
         v_codes = sb.tile([P, DV], U32, name="v_codes", align_bytes=64)
         v_scale = sb.tile([P, DV], U8, name="v_scale", align_bytes=64)
-        nc.vector.quantize_mx(out=v_codes[:].bitcast(FP8X4), scales=v_scale[:], in_=v_bf[:])
-
-        y_acc = ps.tile([NQ, DV], F32, name="y_acc")
-        nc.tensor.matmul_mx(
-            out=y_acc[:],
-            lhsT=w_codes[:].bitcast(FP8X4),
-            lhsT_scale=w_scale[:],
-            rhs=v_codes[:].bitcast(FP8X4),
-            rhs_scale=v_scale[:],
-            start=True,
-            stop=True,
-        )
         y = sb.tile([NQ, DV], F32, name="y")
-        nc.vector.tensor_scalar_mul(y[:], y_acc[:], 1.0 / 16.0)
+        y_acc = [ps.tile([NQ, HALF], F32, name="y_acc%d" % h) for h in range(2)]
+        for h in range(2):
+            cols = slice(h * HALF, (h + 1) * HALF)
+            nc.vector.quantize_mx(
+                out=v_codes[:, cols].bitcast(FP8X4),
+                scales=v_scale[:, cols],
+                in_=v_bf[:, h * HALF * PACK : (h + 1) * HALF * PACK],
+            )
+            nc.tensor.matmul_mx(
+                out=y_acc[h][:],
+                lhsT=w_codes[:].bitcast(FP8X4),
+                lhsT_scale=w_scale[:],
+                rhs=v_codes[:, cols].bitcast(FP8X4),
+                rhs_scale=v_scale[:, cols],
+                start=True,
+                stop=True,
+            )
+        for h in range(2):
+            nc.vector.tensor_scalar_mul(y[:, h * HALF : (h + 1) * HALF], y_acc[h][:], 1.0 / 16.0)
         nc.sync.dma_start(out[0], y[:])

@@ -40,9 +40,9 @@ def tile_attend_silu_kb_topkq128n512t2048_kernel(tc, qT, k_words, k_scales, vT, 
         ps = ctx.enter_context(tc.psum_pool(name="ps", bufs=1))
 
         offsets = sb.tile([P, N // 16], U16, name="offsets")
-        nc.sync.dma_start(offsets[:], offs)
         scale_pool = sb.tile([P, T], U8, name="scale_pool")
         nc.sync.dma_start(scale_pool[:SCALE_ROWS, :].bitcast(I32), k_scales.rearrange("o f t -> f o t").bitcast(I32))
+        nc.sync.dma_start(offsets[:], offs)
         kb_pool = sb.tile([P, T], F32, name="kb_pool")
         vs_pool = sb.tile([P, T], F32, name="vs_pool")
         nc.scalar.dma_start(kb_pool[KB_ROW:, :], kb[0:1, :])

@@ -24,6 +24,9 @@ PASSES = D // (P * PACK)
 KB_ROW = 127
 SCALE_ROWS = 32
 VS_HEAD = 64
+SPREAD_BANKS = 3
+FOLD = SPREAD_BANKS * PACK
+SPREAD = P * FOLD
 V_EARLY = 3 * T // 8
 HALF = DV // 2
 
@@ -45,8 +48,10 @@ def tile_attend_silu_kb_topkq128n512t2048_kernel(tc, qT, k_words, k_scales, vT, 
         nc.sync.dma_start(offsets[:], offs)
         kb_pool = sb.tile([P, T], F32, name="kb_pool")
         vs_pool = sb.tile([P, T], F32, name="vs_pool")
+        vs_fold = sb.tile([P, FOLD], F32, name="vs_fold", tag="runs_then_q", align_bytes=64)
+        nc.scalar.dma_start(vs_fold[:], vs[0, :SPREAD].rearrange("(p c) -> p c", c=FOLD))
         nc.scalar.dma_start(kb_pool[KB_ROW:, :], kb[0:1, :])
-        nc.scalar.dma_start(vs_pool[KB_ROW:, :], vs[0:1, :])
+        nc.scalar.dma_start(vs_pool[KB_ROW:, SPREAD:], vs[0:1, SPREAD:])
 
         word_pool = sb.tile([P, T], I32, name="word_pool")
         nc.sync.dma_start(word_pool[:], k_words[0].rearrange("p t b -> p (t b)").bitcast(I32))
@@ -54,21 +59,31 @@ def tile_attend_silu_kb_topkq128n512t2048_kernel(tc, qT, k_words, k_scales, vT, 
         for o in range(PASSES):
             nc.sync.dma_start(q_raw[:, o], qT[0].rearrange("(o p t) n -> p o t n", o=PASSES, t=PACK)[:, o])
 
+        ident = sb.tile([P, P], F32, name="ident")
+        nc.vector.memset(ident[:], 0.0)
+        make_identity(nc, ident[:], nomemset=True)
         moved = sb.tile([P, PASSES, N], U8, name="moved", align_bytes=64)
         nc.vector.memset(scale_pool[32:64, :].bitcast(I32), 0)
         nc.vector.memset(scale_pool[64:, :].bitcast(I32), 0)
 
         warm_in = sb.tile([P, 1], F32, name="warm_in")
-        nc.gpsimd.memset(warm_in[:], 0.0)
+        nc.vector.memset(warm_in[:], 0.0)
         nc.vector.memset(kb_pool[:KB_ROW, :].bitcast(I32), 0)
-        nc.gpsimd.memset(moved[:].bitcast(I32), 0)
-        ident = sb.tile([P, P], F32, name="ident")
-        nc.vector.memset(ident[:], 0.0)
-        make_identity(nc, ident[:], nomemset=True)
-        nc.vector.memset(vs_pool[:KB_ROW, :VS_HEAD].bitcast(I32), 0)
-        nc.gpsimd.memset(vs_pool[:KB_ROW, VS_HEAD - 8 :].bitcast(I32), 0)
+        nc.vector.memset(moved[:].bitcast(I32), 0)
+        nc.vector.memset(vs_pool[:KB_ROW, SPREAD : SPREAD + VS_HEAD].bitcast(I32), 0)
+        nc.gpsimd.memset(vs_pool[:KB_ROW, SPREAD + VS_HEAD - 8 :].bitcast(I32), 0)
         warm_out = sb.tile([P, 1], F32, name="warm_out")
         nc.scalar.activation(warm_out[:], warm_in[:], ACT.Silu)
+
+        spread = [ps.tile([P, PACK, P], F32, name="spread%d" % b, tag="bank%d" % b) for b in range(SPREAD_BANKS)]
+        for col in range(FOLD):
+            nc.tensor.transpose(spread[col // PACK][:, col % PACK, :], vs_fold[:, col : col + 1].to_broadcast([P, P]), ident[:])
+        for b in range(SPREAD_BANKS):
+            nc.scalar.activation(
+                vs_pool[:, :SPREAD].rearrange("m (p b c) -> m b p c", b=SPREAD_BANKS, c=PACK)[:, b],
+                spread[b][:].rearrange("m c p -> m p c"),
+                ACT.Copy,
+            )
 
         def pick(picked, pool, first, last):
             nc.vector.tensor_copy(
@@ -76,7 +91,7 @@ def tile_attend_silu_kb_topkq128n512t2048_kernel(tc, qT, k_words, k_scales, vT, 
                 pool[:].bitcast(U32).indirect(offsets[:, 2 * first : 2 * last]),
             )
 
-        scale_picked = sb.tile([P, N], U8, name="scale_picked", tag="scales_then_vs")
+        scale_picked = sb.tile([P, N], U8, name="scale_picked")
         nc.vector.tensor_copy(scale_picked[:], scale_pool[:].indirect(offsets[:]))
         kb_picked = sb.tile([P, PACK, P], F32, name="kb_picked")
         pick(kb_picked, kb_pool, 0, 16)
@@ -118,13 +133,13 @@ def tile_attend_silu_kb_topkq128n512t2048_kernel(tc, qT, k_words, k_scales, vT, 
         q_scale = sb.tile([P, PASSES * NQ], U8, name="q_scale", align_bytes=64)
         nc.vector.quantize_mx(out=q_codes[:].bitcast(FP8X4), scales=q_scale[:], in_=q_bf[:].rearrange("p o n t -> p (o n t)"))
 
-        planes = sb.tile([P, PASSES, N], U8, name="planes", align_bytes=64)
+        planes = reuse.tile([P, PASSES, N], U8, name="planes", align_bytes=64, offset=4 * N + 64)
         nc.vector.tensor_copy(
             planes[:].bitcast(I32).rearrange("p o (t j c) -> p o t j c", t=PACK, c=2),
             moved[:].bitcast(I32).rearrange("p o (j t c) -> p o t j c", t=PACK, c=2),
         )
 
-        p_all = sb.tile([P, PACK, NQ], F32, name="p_all")
+        p_all = sb.tile([P, PACK, NQ], F32, name="p_all", tag="p_then_value_codes", align_bytes=64)
         for t in range(PACK):
             acc = ps.tile([P, NQ], F32, name="scores%d" % t, tag="bank%d" % t)
             for o in range(PASSES):
@@ -139,7 +154,7 @@ def tile_attend_silu_kb_topkq128n512t2048_kernel(tc, qT, k_words, k_scales, vT, 
                 )
             nc.scalar.activation(p_all[:, t, :], acc[:], ACT.Silu, bias=kb_col[:, t : t + 1])
 
-        vs_picked = sb.tile([P, PACK, P], F32, name="vs_picked", tag="scales_then_vs")
+        vs_picked = reuse.tile([P, PACK, P], F32, name="vs_picked", offset=0)
         pick(vs_picked, vs_pool, 0, 16)
         vs_turned = ps.tile([P, PACK, P], F32, name="vs_turned")
         for t in range(PACK):
@@ -168,7 +183,7 @@ def tile_attend_silu_kb_topkq128n512t2048_kernel(tc, qT, k_words, k_scales, vT, 
         w_codes = sb.tile([P, NQ], U32, name="w_codes", align_bytes=64)
         w_scale = sb.tile([P, NQ], U8, name="w_scale", align_bytes=64)
         nc.vector.quantize_mx(out=w_codes[:].bitcast(FP8X4), scales=w_scale[:], in_=w_bf[:].rearrange("p q t -> p (q t)"))
-        v_codes = sb.tile([P, DV], U32, name="v_codes", align_bytes=64)
+        v_codes = sb.tile([P, DV], U32, name="v_codes", tag="p_then_value_codes", align_bytes=64)
         v_scale = sb.tile([P, DV], U8, name="v_scale", align_bytes=64)
         y = sb.tile([NQ, DV], F32, name="y")
         y_acc = [ps.tile([NQ, HALF], F32, name="y_acc%d" % h) for h in range(2)]

@@ -21,18 +21,16 @@ MULT = mybir.AluOpType.mult
 P = 128
 PACK = 4
 PASSES = D // (P * PACK)
-KB_ROW = 127
+ROW = 127
 SCALE_ROWS = 32
-VS_HEAD = 64
-SPREAD_BANKS = 3
-FOLD = SPREAD_BANKS * PACK
-SPREAD = P * FOLD
-V_EARLY = 3 * T // 8
 HALF = DV // 2
+V_SPLIT = 18
+VS_HEAD = 576
+AT_V, AT_Q = 0, 4 * T
 
 
-def slot_order(ap):
-    return ap.rearrange("p t (j r) -> p j t r", r=8)
+def by_place(ap):
+    return ap.rearrange("p t m -> p m t")
 
 
 def tile_attend_silu_kb_topkq128n512t2048_kernel(tc, qT, k_words, k_scales, vT, vs, kb, offs, out):
@@ -43,128 +41,98 @@ def tile_attend_silu_kb_topkq128n512t2048_kernel(tc, qT, k_words, k_scales, vT, 
         ps = ctx.enter_context(tc.psum_pool(name="ps", bufs=1))
 
         offsets = sb.tile([P, N // 16], U16, name="offsets")
-        scale_pool = sb.tile([P, T], U8, name="scale_pool")
+        scale_pool = reuse.tile([P, T], U8, name="scale_pool", offset=AT_V)
         nc.sync.dma_start(scale_pool[:SCALE_ROWS, :].bitcast(I32), k_scales.rearrange("o f t -> f o t").bitcast(I32))
         nc.sync.dma_start(offsets[:], offs)
         kb_pool = sb.tile([P, T], F32, name="kb_pool")
+        nc.scalar.dma_start(kb_pool[ROW:, :], kb[0:1, :])
         vs_pool = sb.tile([P, T], F32, name="vs_pool")
-        vs_fold = sb.tile([P, FOLD], F32, name="vs_fold", tag="runs_then_q", align_bytes=64)
-        nc.scalar.dma_start(vs_fold[:], vs[0, :SPREAD].rearrange("(p c) -> p c", c=FOLD))
-        nc.scalar.dma_start(kb_pool[KB_ROW:, :], kb[0:1, :])
-        nc.scalar.dma_start(vs_pool[KB_ROW:, SPREAD:], vs[0:1, SPREAD:])
+        nc.scalar.dma_start(vs_pool[ROW:, :], vs[0:1, :])
 
         word_pool = sb.tile([P, T], I32, name="word_pool")
         nc.sync.dma_start(word_pool[:], k_words[0].rearrange("p t b -> p (t b)").bitcast(I32))
-        q_raw = reuse.tile([P, PASSES, PACK, NQ], F32, name="q_raw", offset=0)
+        q_raw = [reuse.tile([P, PACK, NQ], F32, name="q_raw%d" % o, offset=AT_Q + o * 4 * N) for o in range(PASSES)]
         for o in range(PASSES):
-            nc.sync.dma_start(q_raw[:, o], qT[0].rearrange("(o p t) n -> p o t n", o=PASSES, t=PACK)[:, o])
-
-        ident = sb.tile([P, P], F32, name="ident")
-        nc.vector.memset(ident[:], 0.0)
-        make_identity(nc, ident[:], nomemset=True)
-        moved = sb.tile([P, PASSES, N], U8, name="moved", align_bytes=64)
-        nc.vector.memset(scale_pool[32:64, :].bitcast(I32), 0)
-        nc.vector.memset(scale_pool[64:, :].bitcast(I32), 0)
+            nc.sync.dma_start(q_raw[o][:], qT[0].rearrange("(o p t) n -> p o t n", o=PASSES, t=PACK)[:, o])
 
         warm_in = sb.tile([P, 1], F32, name="warm_in")
         nc.vector.memset(warm_in[:], 0.0)
-        nc.vector.memset(kb_pool[:KB_ROW, :].bitcast(I32), 0)
-        nc.vector.memset(moved[:].bitcast(I32), 0)
-        nc.vector.memset(vs_pool[:KB_ROW, SPREAD : SPREAD + VS_HEAD].bitcast(I32), 0)
-        nc.gpsimd.memset(vs_pool[:KB_ROW, SPREAD + VS_HEAD - 8 :].bitcast(I32), 0)
+        nc.vector.memset(kb_pool[:ROW, :].bitcast(I32), 0)
+        nc.vector.memset(scale_pool[32:64, :].bitcast(I32), 0)
+        nc.vector.memset(scale_pool[64:, :].bitcast(I32), 0)
+        ident = sb.tile([P, P], F32, name="ident")
+        nc.vector.memset(ident[:], 0.0)
+        make_identity(nc, ident[:], nomemset=True)
+        planes = sb.tile([P, PASSES, N], U8, name="planes", align_bytes=64)
+        nc.vector.memset(planes[:].bitcast(I32), 0)
+        nc.vector.memset(vs_pool[:ROW, :VS_HEAD].bitcast(I32), 0)
         warm_out = sb.tile([P, 1], F32, name="warm_out")
         nc.scalar.activation(warm_out[:], warm_in[:], ACT.Silu)
 
-        spread = [ps.tile([P, PACK, P], F32, name="spread%d" % b, tag="bank%d" % b) for b in range(SPREAD_BANKS)]
-        for col in range(FOLD):
-            nc.tensor.transpose(spread[col // PACK][:, col % PACK, :], vs_fold[:, col : col + 1].to_broadcast([P, P]), ident[:])
-        for b in range(SPREAD_BANKS):
-            nc.scalar.activation(
-                vs_pool[:, :SPREAD].rearrange("m (p b c) -> m b p c", b=SPREAD_BANKS, c=PACK)[:, b],
-                spread[b][:].rearrange("m c p -> m p c"),
-                ACT.Copy,
-            )
-
-        def pick(picked, pool, first, last):
-            nc.vector.tensor_copy(
-                slot_order(picked[:].bitcast(U32))[:, first:last],
-                pool[:].bitcast(U32).indirect(offsets[:, 2 * first : 2 * last]),
-            )
-
-        scale_picked = sb.tile([P, N], U8, name="scale_picked")
-        nc.vector.tensor_copy(scale_picked[:], scale_pool[:].indirect(offsets[:]))
-        kb_picked = sb.tile([P, PACK, P], F32, name="kb_picked")
-        pick(kb_picked, kb_pool, 0, 16)
-        v_pool = sb.tile([P, T], F32, name="v_pool")
-        nc.sync.dma_start(v_pool[:, :V_EARLY], vT[:, :V_EARLY])
+        scale_picked = sb.tile([P, PACK, P], U8, name="scale_picked")
+        nc.vector.tensor_copy(by_place(scale_picked[:]), scale_pool[:].indirect(offsets[:]))
         for quad in (0, 2, 1, 3):
             nc.sync.dma_start(
-                moved[32 * quad : 32 * quad + 4].bitcast(I32),
-                scale_picked[8 * quad : 8 * quad + 8, :].bitcast(I32),
+                planes[32 * quad : 32 * quad + 4].bitcast(I32),
+                scale_picked[8 * quad : 8 * quad + 8].rearrange("p t m -> p (t m)").bitcast(I32),
             )
-        nc.sync.dma_start(v_pool[:, V_EARLY:], vT[:, V_EARLY:])
+        nc.vector.memset(vs_pool[:ROW, VS_HEAD:].bitcast(I32), 0)
+        v_pool = reuse.tile([P, T], F32, name="v_pool", offset=AT_V)
+        nc.sync.dma_start(v_pool[:], vT)
 
-        q_bf = sb.tile([P, PASSES, NQ, PACK], BF16, name="q_bf", tag="runs_then_q", align_bytes=64)
+        kb_picked = sb.tile([P, N], F32, name="kb_picked")
+        nc.scalar.activation(kb_picked[:], kb_pool[:].indirect(offsets[:]), ACT.Copy)
+        kb_turned = ps.tile([P, PACK, P], F32, name="kb_turned", tag="kb_then_y")
+        for t in range(PACK):
+            nc.tensor.transpose(kb_turned[:, t, :], kb_picked[:, t::PACK], ident[:])
+
+        words = sb.tile([P, PACK, P], U32, name="words")
+        nc.vector.tensor_copy(by_place(words[:]), word_pool[:].bitcast(U32).indirect(offsets[:]))
+
+        q_bf, q_codes, q_scale, k_codes = [], [], [], []
         for o in range(PASSES):
+            q_bf.append(sb.tile([P, NQ, PACK], BF16, name="q_bf%d" % o, align_bytes=64))
             nc.scalar.activation(
-                q_bf[:, o].rearrange("p (c i) t -> p c t i", i=4),
-                q_raw[:, o].rearrange("p t (c i) -> p c t i", i=4),
+                q_bf[o][:].rearrange("p (c i) t -> p c t i", i=4),
+                q_raw[o][:].rearrange("p t (c i) -> p c t i", i=4),
                 ACT.Copy,
             )
-
-        words = [sb.tile([P, N // 2], U32, name="words%d" % h) for h in range(2)]
-        for h in range(2):
-            nc.vector.tensor_copy(words[h][:], word_pool[:].bitcast(U32).indirect(offsets[:, 16 * h : 16 * h + 16]))
-
-        kb_turned = ps.tile([P, PACK, P], F32, name="kb_turned")
-        for t in range(PACK):
-            nc.tensor.transpose(kb_turned[:, t, :], kb_picked[:, t, :], ident[:])
-        kb_col = reuse.tile([P, PACK], F32, name="kb_col", offset=4 * N)
-        nc.scalar.copy(kb_col[:], kb_turned[:, :, KB_ROW])
-
-        k_codes = sb.tile([P, PACK, PASSES, P], U16, name="k_codes", align_bytes=64)
-        for h in range(2):
-            nc.vector.tensor_copy(
-                k_codes[:, :, :, 64 * h : 64 * h + 64].rearrange("p t o (j r) -> p t o j r", r=8),
-                words[h][:].bitcast(U16).rearrange("p (j t r o) -> p t o j r", t=PACK, r=8, o=PASSES),
-            )
-
-        q_codes = sb.tile([P, PASSES * NQ], U32, name="q_codes", align_bytes=64)
-        q_scale = sb.tile([P, PASSES * NQ], U8, name="q_scale", align_bytes=64)
-        nc.vector.quantize_mx(out=q_codes[:].bitcast(FP8X4), scales=q_scale[:], in_=q_bf[:].rearrange("p o n t -> p (o n t)"))
-
-        planes = reuse.tile([P, PASSES, N], U8, name="planes", align_bytes=64, offset=4 * N + 64)
-        nc.vector.tensor_copy(
-            planes[:].bitcast(I32).rearrange("p o (t j c) -> p o t j c", t=PACK, c=2),
-            moved[:].bitcast(I32).rearrange("p o (j t c) -> p o t j c", t=PACK, c=2),
-        )
+            k_codes.append(sb.tile([P, N], U16, name="k_codes%d" % o, align_bytes=64))
+            nc.vector.tensor_copy(k_codes[o][:], words[:].rearrange("p t m -> p (t m)").bitcast(U16)[:, o::PASSES])
+            q_codes.append(sb.tile([P, NQ], U32, name="q_codes%d" % o, align_bytes=64))
+            q_scale.append(sb.tile([P, NQ], U8, name="q_scale%d" % o, align_bytes=64))
+            nc.vector.quantize_mx(out=q_codes[o][:].bitcast(FP8X4), scales=q_scale[o][:], in_=q_bf[o][:].rearrange("p n t -> p (n t)"))
+        kb_col = reuse.tile([P, PACK], F32, name="kb_col", offset=AT_Q)
+        nc.scalar.copy(kb_col[:], kb_turned[:, :, ROW])
 
         p_all = sb.tile([P, PACK, NQ], F32, name="p_all", tag="p_then_value_codes", align_bytes=64)
-        for t in range(PACK):
-            acc = ps.tile([P, NQ], F32, name="scores%d" % t, tag="bank%d" % t)
-            for o in range(PASSES):
+        acc = [ps.tile([P, NQ], F32, name="scores%d" % t, tag="bank%d" % t) for t in range(PACK)]
+        for o in range(PASSES):
+            for t in range(PACK):
                 nc.tensor.matmul_mx(
-                    out=acc[:],
-                    lhsT=k_codes[:, t, o, :].bitcast(FP4X4),
+                    out=acc[t][:],
+                    lhsT=k_codes[o][:, t * P : (t + 1) * P].bitcast(FP4X4),
                     lhsT_scale=planes[:, o, t * P : (t + 1) * P],
-                    rhs=q_codes[:, o * NQ : (o + 1) * NQ].bitcast(FP8X4),
-                    rhs_scale=q_scale[:, o * NQ : (o + 1) * NQ],
+                    rhs=q_codes[o][:].bitcast(FP8X4),
+                    rhs_scale=q_scale[o][:],
                     start=(o == 0),
                     stop=(o == PASSES - 1),
                 )
-            nc.scalar.activation(p_all[:, t, :], acc[:], ACT.Silu, bias=kb_col[:, t : t + 1])
+        for t in range(PACK):
+            nc.scalar.activation(p_all[:, t, :], acc[t][:], ACT.Silu, bias=kb_col[:, t : t + 1])
 
-        vs_picked = reuse.tile([P, PACK, P], F32, name="vs_picked", offset=0)
-        pick(vs_picked, vs_pool, 0, 16)
-        vs_turned = ps.tile([P, PACK, P], F32, name="vs_turned")
+        vs_picked = reuse.tile([P, PACK, P], F32, name="vs_picked", offset=AT_Q + 4 * N)
+        nc.vector.tensor_copy(by_place(vs_picked[:].bitcast(U32)), vs_pool[:].bitcast(U32).indirect(offsets[:]))
+        vs_turned = ps.tile([P, PACK, P], F32, name="vs_turned", tag="bank0")
         for t in range(PACK):
             nc.tensor.transpose(vs_turned[:, t, :], vs_picked[:, t, :], ident[:])
 
-        v_picked = sb.tile([P, 2, P, 2], BF16, name="v_picked", tag="runs_then_q", align_bytes=64)
-        nc.vector.tensor_copy(v_picked[:].rearrange("p u (j r) e -> p j u e r", r=8), v_pool[:].indirect(offsets[:]))
-        v_turned = ps.tile([P, 2, DV], F32, name="v_turned", tag="bank0")
+        v_picked = reuse.tile([P, N], BF16, name="v_picked", offset=AT_Q)
+        nc.vector.tensor_copy(v_picked[:, : 16 * V_SPLIT], v_pool[:].indirect(offsets[:, :V_SPLIT]))
+        nc.scalar.activation(v_picked[:, 16 * V_SPLIT :], v_pool[:].indirect(offsets[:, V_SPLIT:]), ACT.Copy)
+        v_turned = ps.tile([P, 2, DV], F32, name="v_turned")
         for u in range(2):
-            nc.tensor.transpose(v_turned[:, u, :], v_picked[:, u].rearrange("p m e -> p (m e)").bitcast(F32), ident[:])
+            nc.tensor.transpose(v_turned[:, u, :], v_picked[:].bitcast(F32)[:, u::2], ident[:])
         v_bf = sb.tile([P, DV * PACK], BF16, name="v_bf", align_bytes=64)
         for h in range(2):
             nc.scalar.copy(
@@ -172,11 +140,11 @@ def tile_attend_silu_kb_topkq128n512t2048_kernel(tc, qT, k_words, k_scales, vT, 
                 v_turned[:].rearrange("p u c -> p c u")[:, h * HALF : (h + 1) * HALF],
             )
 
-        w_bf = sb.tile([P, NQ, PACK], BF16, name="w_bf", align_bytes=64)
+        w_bf = reuse.tile([P, NQ, PACK], BF16, name="w_bf", align_bytes=64, offset=AT_V)
         nc.vector.tensor_tensor(
             w_bf[:].rearrange("p (c i) t -> p c t i", i=4),
             p_all[:].rearrange("p t (c i) -> p c t i", i=4),
-            vs_turned[:, :, KB_ROW:].unsqueeze(1).to_broadcast([P, NQ // 4, PACK, 4]),
+            vs_turned[:, :, ROW:].unsqueeze(1).to_broadcast([P, NQ // 4, PACK, 4]),
             MULT,
         )
 
@@ -186,7 +154,7 @@ def tile_attend_silu_kb_topkq128n512t2048_kernel(tc, qT, k_words, k_scales, vT, 
         v_codes = sb.tile([P, DV], U32, name="v_codes", tag="p_then_value_codes", align_bytes=64)
         v_scale = sb.tile([P, DV], U8, name="v_scale", align_bytes=64)
         y = sb.tile([NQ, DV], F32, name="y")
-        y_acc = [ps.tile([NQ, HALF], F32, name="y_acc%d" % h) for h in range(2)]
+        y_acc = [ps.tile([NQ, HALF], F32, name="y_acc0", tag="kb_then_y"), ps.tile([NQ, HALF], F32, name="y_acc1")]
         for h in range(2):
             cols = slice(h * HALF, (h + 1) * HALF)
             nc.vector.quantize_mx(

@@ -26,11 +26,11 @@ SCALE_ROWS = 32
 HALF = DV // 2
 V_SPLIT = 18
 VS_HEAD = 576
-AT_V, AT_Q = 0, 4 * T
+AT_V, AT_Q, AT_KB = 0, 4 * T, 6 * T
 
 
 def by_place(ap):
-    return ap.rearrange("p t m -> p m t")
+    return ap.rearrange("p t (j r) -> p j t r", r=8)
 
 
 def tile_attend_silu_kb_topkq128n512t2048_kernel(tc, qT, k_words, k_scales, vT, vs, kb, offs, out):
@@ -80,18 +80,20 @@ def tile_attend_silu_kb_topkq128n512t2048_kernel(tc, qT, k_words, k_scales, vT, 
         v_pool = reuse.tile([P, T], F32, name="v_pool", offset=AT_V)
         nc.sync.dma_start(v_pool[:], vT)
 
-        kb_picked = sb.tile([P, N], F32, name="kb_picked")
-        nc.scalar.activation(kb_picked[:], kb_pool[:].indirect(offsets[:]), ACT.Copy)
+        kb_listed = reuse.tile([P, N], F32, name="kb_listed", offset=AT_KB)
+        nc.scalar.activation(kb_listed[:], kb_pool[:].indirect(offsets[:]), ACT.Copy)
+        kb_picked = sb.tile([P, PACK, P], F32, name="kb_picked")
+        nc.scalar.copy(by_place(kb_picked[:]), kb_listed[:].rearrange("p (j t r) -> p j t r", t=PACK, r=8))
         kb_turned = ps.tile([P, PACK, P], F32, name="kb_turned", tag="kb_then_y")
         for t in range(PACK):
-            nc.tensor.transpose(kb_turned[:, t, :], kb_picked[:, t::PACK], ident[:])
+            nc.tensor.transpose(kb_turned[:, t, :], kb_picked[:, t, :], ident[:])
 
         words = sb.tile([P, PACK, P], U32, name="words")
         nc.vector.tensor_copy(by_place(words[:]), word_pool[:].bitcast(U32).indirect(offsets[:]))
 
         q_bf, q_codes, q_scale, k_codes = [], [], [], []
         for o in range(PASSES):
-            q_bf.append(sb.tile([P, NQ, PACK], BF16, name="q_bf%d" % o, align_bytes=64))
+            q_bf.append(reuse.tile([P, NQ, PACK], BF16, name="q_bf%d" % o, align_bytes=64, offset=AT_KB + o * 2 * N))
             nc.scalar.activation(
                 q_bf[o][:].rearrange("p (c i) t -> p c t i", i=4),
                 q_raw[o][:].rearrange("p t (c i) -> p c t i", i=4),
@@ -128,8 +130,9 @@ def tile_attend_silu_kb_topkq128n512t2048_kernel(tc, qT, k_words, k_scales, vT, 
             nc.tensor.transpose(vs_turned[:, t, :], vs_picked[:, t, :], ident[:])
 
         v_picked = reuse.tile([P, N], BF16, name="v_picked", offset=AT_Q)
-        nc.vector.tensor_copy(v_picked[:, : 16 * V_SPLIT], v_pool[:].indirect(offsets[:, :V_SPLIT]))
-        nc.scalar.activation(v_picked[:, 16 * V_SPLIT :], v_pool[:].indirect(offsets[:, V_SPLIT:]), ACT.Copy)
+        v_slots = v_picked[:].rearrange("p (j r t) -> p j t r", t=PACK, r=8)
+        nc.vector.tensor_copy(v_slots[:, : V_SPLIT // 2], v_pool[:].indirect(offsets[:, :V_SPLIT]))
+        nc.scalar.activation(v_slots[:, V_SPLIT // 2 :], v_pool[:].indirect(offsets[:, V_SPLIT:]), ACT.Copy)
         v_turned = ps.tile([P, 2, DV], F32, name="v_turned")
         for u in range(2):
             nc.tensor.transpose(v_turned[:, u, :], v_picked[:].bitcast(F32)[:, u::2], ident[:])

@@ -25,7 +25,7 @@ ROW = 127
 SCALE_ROWS = 32
 HALF = DV // 2
 V_SPLIT = 18
-VS_HEAD = 576
+V_EARLY = T // 4
 AT_V, AT_Q, AT_KB = 0, 4 * T, 6 * T
 
 
@@ -41,7 +41,7 @@ def tile_attend_silu_kb_topkq128n512t2048_kernel(tc, qT, k_words, k_scales, vT, 
         ps = ctx.enter_context(tc.psum_pool(name="ps", bufs=1))
 
         offsets = sb.tile([P, N // 16], U16, name="offsets")
-        scale_pool = reuse.tile([P, T], U8, name="scale_pool", offset=AT_V)
+        scale_pool = sb.tile([P, T], U8, name="scale_pool")
         nc.sync.dma_start(scale_pool[:SCALE_ROWS, :].bitcast(I32), k_scales.rearrange("o f t -> f o t").bitcast(I32))
         nc.sync.dma_start(offsets[:], offs)
         kb_pool = sb.tile([P, T], F32, name="kb_pool")
@@ -49,11 +49,13 @@ def tile_attend_silu_kb_topkq128n512t2048_kernel(tc, qT, k_words, k_scales, vT, 
         vs_pool = sb.tile([P, T], F32, name="vs_pool")
         nc.scalar.dma_start(vs_pool[ROW:, :], vs[0:1, :])
 
-        word_pool = sb.tile([P, T], I32, name="word_pool")
+        word_pool = sb.tile([P, T], I32, name="word_pool", align_bytes=256)
         nc.sync.dma_start(word_pool[:], k_words[0].rearrange("p t b -> p (t b)").bitcast(I32))
-        q_raw = [reuse.tile([P, PACK, NQ], F32, name="q_raw%d" % o, offset=AT_Q + o * 4 * N) for o in range(PASSES)]
+        q_raw = [reuse.tile([P, PACK, NQ], F32, name="q_raw%d" % o, align_bytes=256, offset=AT_Q + o * 4 * N) for o in range(PASSES)]
         for o in range(PASSES):
             nc.sync.dma_start(q_raw[o][:], qT[0].rearrange("(o p t) n -> p o t n", o=PASSES, t=PACK)[:, o])
+        v_pool = reuse.tile([P, T], F32, name="v_pool", align_bytes=256, offset=AT_V)
+        nc.sync.dma_start(v_pool[:, :V_EARLY], vT[:, :V_EARLY])
 
         warm_in = sb.tile([P, 1], F32, name="warm_in")
         nc.vector.memset(warm_in[:], 0.0)
@@ -65,7 +67,6 @@ def tile_attend_silu_kb_topkq128n512t2048_kernel(tc, qT, k_words, k_scales, vT, 
         make_identity(nc, ident[:], nomemset=True)
         planes = sb.tile([P, PASSES, N], U8, name="planes", align_bytes=64)
         nc.vector.memset(planes[:].bitcast(I32), 0)
-        nc.vector.memset(vs_pool[:ROW, :VS_HEAD].bitcast(I32), 0)
         warm_out = sb.tile([P, 1], F32, name="warm_out")
         nc.scalar.activation(warm_out[:], warm_in[:], ACT.Silu)
 
@@ -76,9 +77,8 @@ def tile_attend_silu_kb_topkq128n512t2048_kernel(tc, qT, k_words, k_scales, vT, 
                 planes[32 * quad : 32 * quad + 4].bitcast(I32),
                 scale_picked[8 * quad : 8 * quad + 8].rearrange("p t m -> p (t m)").bitcast(I32),
             )
-        nc.vector.memset(vs_pool[:ROW, VS_HEAD:].bitcast(I32), 0)
-        v_pool = reuse.tile([P, T], F32, name="v_pool", offset=AT_V)
-        nc.sync.dma_start(v_pool[:], vT)
+        nc.vector.memset(vs_pool[:ROW, :].bitcast(I32), 0)
+        nc.sync.dma_start(v_pool[:, V_EARLY:], vT[:, V_EARLY:])
 
         kb_listed = reuse.tile([P, N], F32, name="kb_listed", offset=AT_KB)
         nc.scalar.activation(kb_listed[:], kb_pool[:].indirect(offsets[:]), ACT.Copy)

@@ -24,13 +24,16 @@ PASSES = D // (P * PACK)
 ROW = 127
 SCALE_ROWS = 32
 HALF = DV // 2
-V_SPLIT = 18
-V_EARLY = T // 4
-AT_V, AT_Q, AT_KB = 0, 4 * T, 6 * T
+VS_HEAD = 256
+VS_SPLIT = 24
+V_SPLIT = 24
+AT_SCALE = 0
+AT_V = AT_SCALE + PASSES * N
+AT_Q = AT_V + 4 * T
 
 
 def by_place(ap):
-    return ap.rearrange("p t (j r) -> p j t r", r=8)
+    return ap.rearrange("p t m -> p m t")
 
 
 def tile_attend_silu_kb_topkq128n512t2048_kernel(tc, qT, k_words, k_scales, vT, vs, kb, offs, out):
@@ -41,12 +44,12 @@ def tile_attend_silu_kb_topkq128n512t2048_kernel(tc, qT, k_words, k_scales, vT, 
         ps = ctx.enter_context(tc.psum_pool(name="ps", bufs=1))
 
         offsets = sb.tile([P, N // 16], U16, name="offsets")
-        scale_pool = sb.tile([P, T], U8, name="scale_pool")
+        scale_pool = reuse.tile([P, T], U8, name="scale_pool", align_bytes=256, offset=AT_SCALE)
         nc.sync.dma_start(scale_pool[:SCALE_ROWS, :].bitcast(I32), k_scales.rearrange("o f t -> f o t").bitcast(I32))
         nc.sync.dma_start(offsets[:], offs)
-        kb_pool = sb.tile([P, T], F32, name="kb_pool")
+        kb_pool = sb.tile([P, T], F32, name="kb_pool", align_bytes=256)
+        vs_pool = sb.tile([P, T], F32, name="vs_pool", align_bytes=256)
         nc.scalar.dma_start(kb_pool[ROW:, :], kb[0:1, :])
-        vs_pool = sb.tile([P, T], F32, name="vs_pool")
         nc.scalar.dma_start(vs_pool[ROW:, :], vs[0:1, :])
 
         word_pool = sb.tile([P, T], I32, name="word_pool", align_bytes=256)
@@ -54,58 +57,73 @@ def tile_attend_silu_kb_topkq128n512t2048_kernel(tc, qT, k_words, k_scales, vT, 
         q_raw = [reuse.tile([P, PACK, NQ], F32, name="q_raw%d" % o, align_bytes=256, offset=AT_Q + o * 4 * N) for o in range(PASSES)]
         for o in range(PASSES):
             nc.sync.dma_start(q_raw[o][:], qT[0].rearrange("(o p t) n -> p o t n", o=PASSES, t=PACK)[:, o])
-        v_pool = reuse.tile([P, T], F32, name="v_pool", align_bytes=256, offset=AT_V)
-        nc.sync.dma_start(v_pool[:, :V_EARLY], vT[:, :V_EARLY])
 
+        nc.vector.memset(scale_pool[32:64, :].bitcast(I32), 0)
+        nc.vector.memset(scale_pool[64:, :].bitcast(I32), 0)
         warm_in = sb.tile([P, 1], F32, name="warm_in")
         nc.vector.memset(warm_in[:], 0.0)
         nc.vector.memset(kb_pool[:ROW, :].bitcast(I32), 0)
-        nc.vector.memset(scale_pool[32:64, :].bitcast(I32), 0)
-        nc.vector.memset(scale_pool[64:, :].bitcast(I32), 0)
+        nc.vector.memset(vs_pool[:ROW, :VS_HEAD].bitcast(I32), 0)
         ident = sb.tile([P, P], F32, name="ident")
         nc.vector.memset(ident[:], 0.0)
         make_identity(nc, ident[:], nomemset=True)
-        planes = sb.tile([P, PASSES, N], U8, name="planes", align_bytes=64)
-        nc.vector.memset(planes[:].bitcast(I32), 0)
         warm_out = sb.tile([P, 1], F32, name="warm_out")
         nc.scalar.activation(warm_out[:], warm_in[:], ACT.Silu)
 
-        scale_picked = sb.tile([P, PACK, P], U8, name="scale_picked")
+        scale_picked = sb.tile([P, PACK, P], U8, name="scale_picked", align_bytes=256)
         nc.vector.tensor_copy(by_place(scale_picked[:]), scale_pool[:].indirect(offsets[:]))
+        planes = reuse.tile([P, PASSES, N], U8, name="planes", align_bytes=256, offset=AT_SCALE)
         for quad in (0, 2, 1, 3):
             nc.sync.dma_start(
                 planes[32 * quad : 32 * quad + 4].bitcast(I32),
                 scale_picked[8 * quad : 8 * quad + 8].rearrange("p t m -> p (t m)").bitcast(I32),
             )
-        nc.vector.memset(vs_pool[:ROW, :].bitcast(I32), 0)
-        nc.sync.dma_start(v_pool[:, V_EARLY:], vT[:, V_EARLY:])
+        v_pool = reuse.tile([P, T], F32, name="v_pool", align_bytes=256, offset=AT_V)
+        nc.sync.dma_start(v_pool[:], vT)
+        nc.vector.memset(vs_pool[:ROW, VS_HEAD:].bitcast(I32), 0)
 
-        kb_listed = reuse.tile([P, N], F32, name="kb_listed", offset=AT_KB)
-        nc.scalar.activation(kb_listed[:], kb_pool[:].indirect(offsets[:]), ACT.Copy)
-        kb_picked = sb.tile([P, PACK, P], F32, name="kb_picked")
-        nc.scalar.copy(by_place(kb_picked[:]), kb_listed[:].rearrange("p (j t r) -> p j t r", t=PACK, r=8))
+        kb_picked = sb.tile([P, N], F32, name="kb_picked")
+        nc.scalar.activation(kb_picked[:], kb_pool[:].indirect(offsets[:]), ACT.Copy)
         kb_turned = ps.tile([P, PACK, P], F32, name="kb_turned", tag="kb_then_y")
         for t in range(PACK):
-            nc.tensor.transpose(kb_turned[:, t, :], kb_picked[:, t, :], ident[:])
+            nc.tensor.transpose(kb_turned[:, t, :], kb_picked[:, t::PACK], ident[:])
 
         words = sb.tile([P, PACK, P], U32, name="words")
         nc.vector.tensor_copy(by_place(words[:]), word_pool[:].bitcast(U32).indirect(offsets[:]))
 
-        q_bf, q_codes, q_scale, k_codes = [], [], [], []
-        for o in range(PASSES):
-            q_bf.append(reuse.tile([P, NQ, PACK], BF16, name="q_bf%d" % o, align_bytes=64, offset=AT_KB + o * 2 * N))
+        q_bf = [sb.tile([P, NQ, PACK], BF16, name="q_bf%d" % o, align_bytes=64) for o in range(PASSES)]
+        q_codes = [sb.tile([P, NQ], U32, name="q_codes%d" % o, align_bytes=64) for o in range(PASSES)]
+        q_scale = [sb.tile([P, NQ], U8, name="q_scale%d" % o, align_bytes=64) for o in range(PASSES)]
+        k_first = sb.tile([P, P], U16, name="k_first", align_bytes=64)
+        k_rest = sb.tile([P, N - P], U16, name="k_rest", align_bytes=64)
+        k_second = sb.tile([P, N], U16, name="k_second", align_bytes=64)
+        k_codes = [
+            [k_first[:]] + [k_rest[:, t * P : (t + 1) * P] for t in range(PACK - 1)],
+            [k_second[:, t * P : (t + 1) * P] for t in range(PACK)],
+        ]
+        halves_of_words = words[:].rearrange("p t m -> p (t m)").bitcast(U16)
+
+        def quantise_q(o):
             nc.scalar.activation(
                 q_bf[o][:].rearrange("p (c i) t -> p c t i", i=4),
                 q_raw[o][:].rearrange("p t (c i) -> p c t i", i=4),
                 ACT.Copy,
             )
-            k_codes.append(sb.tile([P, N], U16, name="k_codes%d" % o, align_bytes=64))
-            nc.vector.tensor_copy(k_codes[o][:], words[:].rearrange("p t m -> p (t m)").bitcast(U16)[:, o::PASSES])
-            q_codes.append(sb.tile([P, NQ], U32, name="q_codes%d" % o, align_bytes=64))
-            q_scale.append(sb.tile([P, NQ], U8, name="q_scale%d" % o, align_bytes=64))
             nc.vector.quantize_mx(out=q_codes[o][:].bitcast(FP8X4), scales=q_scale[o][:], in_=q_bf[o][:].rearrange("p n t -> p (n t)"))
+
+        quantise_q(0)
         kb_col = reuse.tile([P, PACK], F32, name="kb_col", offset=AT_Q)
-        nc.scalar.copy(kb_col[:], kb_turned[:, :, ROW])
+        nc.vector.tensor_copy(kb_col[:], kb_turned[:, :, ROW])
+        nc.vector.tensor_copy(k_first[:], halves_of_words[:, 0 : PASSES * P : PASSES])
+        nc.vector.tensor_copy(k_rest[:], halves_of_words[:, PASSES * P :: PASSES])
+        nc.vector.tensor_copy(k_second[:], halves_of_words[:, 1::PASSES])
+        quantise_q(1)
+
+        vs_picked = reuse.tile([P, N], F32, name="vs_picked", offset=AT_Q + 4 * N)
+        nc.scalar.activation(vs_picked[:, : 16 * VS_SPLIT], vs_pool[:].indirect(offsets[:, :VS_SPLIT]), ACT.Copy)
+        nc.vector.tensor_copy(vs_picked[:, 16 * VS_SPLIT :], vs_pool[:].indirect(offsets[:, VS_SPLIT:]))
+        vs_col = sb.tile([P, PACK, 1], F32, name="vs_col")
+        nc.sync.dma_start(vs_col[:, :, 0], vs_picked[ROW:, :].rearrange("r (p t) -> r p t", t=PACK))
 
         p_all = sb.tile([P, PACK, NQ], F32, name="p_all", tag="p_then_value_codes", align_bytes=64)
         acc = [ps.tile([P, NQ], F32, name="scores%d" % t, tag="bank%d" % t) for t in range(PACK)]
@@ -113,7 +131,7 @@ def tile_attend_silu_kb_topkq128n512t2048_kernel(tc, qT, k_words, k_scales, vT, 
             for t in range(PACK):
                 nc.tensor.matmul_mx(
                     out=acc[t][:],
-                    lhsT=k_codes[o][:, t * P : (t + 1) * P].bitcast(FP4X4),
+                    lhsT=k_codes[o][t].bitcast(FP4X4),
                     lhsT_scale=planes[:, o, t * P : (t + 1) * P],
                     rhs=q_codes[o][:].bitcast(FP8X4),
                     rhs_scale=q_scale[o][:],
@@ -123,19 +141,13 @@ def tile_attend_silu_kb_topkq128n512t2048_kernel(tc, qT, k_words, k_scales, vT, 
         for t in range(PACK):
             nc.scalar.activation(p_all[:, t, :], acc[t][:], ACT.Silu, bias=kb_col[:, t : t + 1])
 
-        vs_picked = reuse.tile([P, PACK, P], F32, name="vs_picked", offset=AT_Q + 4 * N)
-        nc.vector.tensor_copy(by_place(vs_picked[:].bitcast(U32)), vs_pool[:].bitcast(U32).indirect(offsets[:]))
-        vs_turned = ps.tile([P, PACK, P], F32, name="vs_turned", tag="bank0")
-        for t in range(PACK):
-            nc.tensor.transpose(vs_turned[:, t, :], vs_picked[:, t, :], ident[:])
-
-        v_picked = reuse.tile([P, N], BF16, name="v_picked", offset=AT_Q)
-        v_slots = v_picked[:].rearrange("p (j r t) -> p j t r", t=PACK, r=8)
-        nc.vector.tensor_copy(v_slots[:, : V_SPLIT // 2], v_pool[:].indirect(offsets[:, :V_SPLIT]))
-        nc.scalar.activation(v_slots[:, V_SPLIT // 2 :], v_pool[:].indirect(offsets[:, V_SPLIT:]), ACT.Copy)
+        v_picked = sb.tile([P, 2, P, 2], BF16, name="v_picked")
+        v_slots = v_picked[:].rearrange("p u m e -> p m u e")
+        nc.vector.tensor_copy(v_slots[:, : 4 * V_SPLIT], v_pool[:].indirect(offsets[:, :V_SPLIT]))
+        nc.scalar.activation(v_slots[:, 4 * V_SPLIT :], v_pool[:].indirect(offsets[:, V_SPLIT:]), ACT.Copy)
         v_turned = ps.tile([P, 2, DV], F32, name="v_turned")
         for u in range(2):
-            nc.tensor.transpose(v_turned[:, u, :], v_picked[:].bitcast(F32)[:, u::2], ident[:])
+            nc.tensor.transpose(v_turned[:, u, :], v_picked[:, u].rearrange("p m e -> p (m e)").bitcast(F32), ident[:])
         v_bf = sb.tile([P, DV * PACK], BF16, name="v_bf", align_bytes=64)
         for h in range(2):
             nc.scalar.copy(
@@ -144,16 +156,20 @@ def tile_attend_silu_kb_topkq128n512t2048_kernel(tc, qT, k_words, k_scales, vT, 
             )
 
         w_bf = reuse.tile([P, NQ, PACK], BF16, name="w_bf", align_bytes=64, offset=AT_V)
-        nc.vector.tensor_tensor(
-            w_bf[:].rearrange("p (c i) t -> p c t i", i=4),
-            p_all[:].rearrange("p t (c i) -> p c t i", i=4),
-            vs_turned[:, :, ROW:].unsqueeze(1).to_broadcast([P, NQ // 4, PACK, 4]),
-            MULT,
-        )
-
         w_codes = sb.tile([P, NQ], U32, name="w_codes", align_bytes=64)
         w_scale = sb.tile([P, NQ], U8, name="w_scale", align_bytes=64)
-        nc.vector.quantize_mx(out=w_codes[:].bitcast(FP8X4), scales=w_scale[:], in_=w_bf[:].rearrange("p q t -> p (q t)"))
+        halves = [slice(h * NQ // 2, (h + 1) * NQ // 2) for h in range(2)]
+        for rows in halves:
+            nc.vector.tensor_tensor(
+                w_bf[:, rows].rearrange("p (c i) t -> p c t i", i=4),
+                p_all[:, :, rows].rearrange("p t (c i) -> p c t i", i=4),
+                vs_col[:].unsqueeze(1).to_broadcast([P, NQ // 8, PACK, 4]),
+                MULT,
+            )
+        for rows in halves:
+            nc.vector.quantize_mx(
+                out=w_codes[:, rows].bitcast(FP8X4), scales=w_scale[:, rows], in_=w_bf[:, rows].rearrange("p q t -> p (q t)")
+            )
         v_codes = sb.tile([P, DV], U32, name="v_codes", tag="p_then_value_codes", align_bytes=64)
         v_scale = sb.tile([P, DV], U8, name="v_scale", align_bytes=64)
         y = sb.tile([NQ, DV], F32, name="y")

@@ -25,10 +25,11 @@ ROW = 127
 SCALE_ROWS = 32
 HALF = DV // 2
 VS_HEAD = 256
+V_EARLY = 3 * T // 8
 VS_SPLIT = 24
 V_SPLIT = 24
 AT_SCALE = 0
-AT_V = AT_SCALE + PASSES * N
+AT_V = AT_SCALE + T
 AT_Q = AT_V + 4 * T
 
 
@@ -57,6 +58,8 @@ def tile_attend_silu_kb_topkq128n512t2048_kernel(tc, qT, k_words, k_scales, vT, 
         q_raw = [reuse.tile([P, PACK, NQ], F32, name="q_raw%d" % o, align_bytes=256, offset=AT_Q + o * 4 * N) for o in range(PASSES)]
         for o in range(PASSES):
             nc.sync.dma_start(q_raw[o][:], qT[0].rearrange("(o p t) n -> p o t n", o=PASSES, t=PACK)[:, o])
+        v_pool = reuse.tile([P, T], F32, name="v_pool", align_bytes=256, offset=AT_V)
+        nc.sync.dma_start(v_pool[:, :V_EARLY], vT[:, :V_EARLY])
 
         nc.vector.memset(scale_pool[32:64, :].bitcast(I32), 0)
         nc.vector.memset(scale_pool[64:, :].bitcast(I32), 0)
@@ -78,8 +81,7 @@ def tile_attend_silu_kb_topkq128n512t2048_kernel(tc, qT, k_words, k_scales, vT, 
                 planes[32 * quad : 32 * quad + 4].bitcast(I32),
                 scale_picked[8 * quad : 8 * quad + 8].rearrange("p t m -> p (t m)").bitcast(I32),
             )
-        v_pool = reuse.tile([P, T], F32, name="v_pool", align_bytes=256, offset=AT_V)
-        nc.sync.dma_start(v_pool[:], vT)
+        nc.sync.dma_start(v_pool[:, V_EARLY:], vT[:, V_EARLY:])
         nc.vector.memset(vs_pool[:ROW, VS_HEAD:].bitcast(I32), 0)
 
         kb_picked = sb.tile([P, N], F32, name="kb_picked")

@@ -24,8 +24,8 @@ PASSES = D // (P * PACK)
 ROW = 127
 SCALE_ROWS = 32
 HALF = DV // 2
-VS_HEAD = 256
-V_EARLY = 3 * T // 8
+VS_HEAD = 640
+V_EARLY = T // 4
 VS_SPLIT = 24
 V_SPLIT = 24
 AT_SCALE = 0

@@ -24,9 +24,11 @@ PASSES = D // (P * PACK)
 ROW = 127
 SCALE_ROWS = 32
 HALF = DV // 2
-VS_HEAD = 640
+VS_HEAD = 256
+VS_TAIL = 1280
+VS_OVERLAP = 8
 V_EARLY = T // 4
-VS_SPLIT = 24
+VS_SPLIT = 20
 V_SPLIT = 24
 AT_SCALE = 0
 AT_V = AT_SCALE + T
@@ -61,15 +63,16 @@ def tile_attend_silu_kb_topkq128n512t2048_kernel(tc, qT, k_words, k_scales, vT, 
         v_pool = reuse.tile([P, T], F32, name="v_pool", align_bytes=256, offset=AT_V)
         nc.sync.dma_start(v_pool[:, :V_EARLY], vT[:, :V_EARLY])
 
+        ident = sb.tile([P, P], F32, name="ident")
+        nc.vector.memset(ident[:], 0.0)
+        make_identity(nc, ident[:], nomemset=True)
         nc.vector.memset(scale_pool[32:64, :].bitcast(I32), 0)
         nc.vector.memset(scale_pool[64:, :].bitcast(I32), 0)
         warm_in = sb.tile([P, 1], F32, name="warm_in")
         nc.vector.memset(warm_in[:], 0.0)
         nc.vector.memset(kb_pool[:ROW, :].bitcast(I32), 0)
         nc.vector.memset(vs_pool[:ROW, :VS_HEAD].bitcast(I32), 0)
-        ident = sb.tile([P, P], F32, name="ident")
-        nc.vector.memset(ident[:], 0.0)
-        make_identity(nc, ident[:], nomemset=True)
+        nc.gpsimd.memset(vs_pool[:ROW, VS_HEAD - VS_OVERLAP : VS_TAIL].bitcast(I32), 0)
         warm_out = sb.tile([P, 1], F32, name="warm_out")
         nc.scalar.activation(warm_out[:], warm_in[:], ACT.Silu)
 
@@ -82,7 +85,7 @@ def tile_attend_silu_kb_topkq128n512t2048_kernel(tc, qT, k_words, k_scales, vT, 
                 scale_picked[8 * quad : 8 * quad + 8].rearrange("p t m -> p (t m)").bitcast(I32),
             )
         nc.sync.dma_start(v_pool[:, V_EARLY:], vT[:, V_EARLY:])
-        nc.vector.memset(vs_pool[:ROW, VS_HEAD:].bitcast(I32), 0)
+        nc.vector.memset(vs_pool[:ROW, VS_TAIL:].bitcast(I32), 0)
 
         kb_picked = sb.tile([P, N], F32, name="kb_picked")
         nc.scalar.activation(kb_picked[:], kb_pool[:].indirect(offsets[:]), ACT.Copy)

@@ -28,11 +28,12 @@ VS_HEAD = 256
 VS_TAIL = 1280
 VS_OVERLAP = 8
 V_EARLY = T // 4
-VS_SPLIT = 20
+VS_SPLIT = 24
 V_SPLIT = 24
 AT_SCALE = 0
 AT_V = AT_SCALE + T
-AT_Q = AT_V + 4 * T
+AT_WORDS = AT_V + 4 * T
+AT_Q = AT_WORDS + 4 * T
 
 
 def by_place(ap):
@@ -55,7 +56,7 @@ def tile_attend_silu_kb_topkq128n512t2048_kernel(tc, qT, k_words, k_scales, vT, 
         nc.scalar.dma_start(kb_pool[ROW:, :], kb[0:1, :])
         nc.scalar.dma_start(vs_pool[ROW:, :], vs[0:1, :])
 
-        word_pool = sb.tile([P, T], I32, name="word_pool", align_bytes=256)
+        word_pool = reuse.tile([P, T], I32, name="word_pool", align_bytes=256, offset=AT_WORDS)
         nc.sync.dma_start(word_pool[:], k_words[0].rearrange("p t b -> p (t b)").bitcast(I32))
         q_raw = [reuse.tile([P, PACK, NQ], F32, name="q_raw%d" % o, align_bytes=256, offset=AT_Q + o * 4 * N) for o in range(PASSES)]
         for o in range(PASSES):
@@ -97,14 +98,14 @@ def tile_attend_silu_kb_topkq128n512t2048_kernel(tc, qT, k_words, k_scales, vT, 
         nc.vector.tensor_copy(by_place(words[:]), word_pool[:].bitcast(U32).indirect(offsets[:]))
 
         q_bf = [sb.tile([P, NQ, PACK], BF16, name="q_bf%d" % o, align_bytes=64) for o in range(PASSES)]
-        q_codes = [sb.tile([P, NQ], U32, name="q_codes%d" % o, align_bytes=64) for o in range(PASSES)]
+        q_codes = [reuse.tile([P, NQ], U32, name="q_codes%d" % o, align_bytes=64, offset=AT_WORDS + o * 4 * NQ) for o in range(PASSES)]
         q_scale = [sb.tile([P, NQ], U8, name="q_scale%d" % o, align_bytes=64) for o in range(PASSES)]
         k_first = sb.tile([P, P], U16, name="k_first", align_bytes=64)
         k_rest = sb.tile([P, N - P], U16, name="k_rest", align_bytes=64)
-        k_second = sb.tile([P, N], U16, name="k_second", align_bytes=64)
+        k_second = [sb.tile([P, N // 2], U16, name="k_second%d" % h, align_bytes=64) for h in range(2)]
         k_codes = [
             [k_first[:]] + [k_rest[:, t * P : (t + 1) * P] for t in range(PACK - 1)],
-            [k_second[:, t * P : (t + 1) * P] for t in range(PACK)],
+            [k_second[t // 2][:, t % 2 * P : (t % 2 + 1) * P] for t in range(PACK)],
         ]
         halves_of_words = words[:].rearrange("p t m -> p (t m)").bitcast(U16)
 
@@ -116,19 +117,22 @@ def tile_attend_silu_kb_topkq128n512t2048_kernel(tc, qT, k_words, k_scales, vT, 
             )
             nc.vector.quantize_mx(out=q_codes[o][:].bitcast(FP8X4), scales=q_scale[o][:], in_=q_bf[o][:].rearrange("p n t -> p (n t)"))
 
-        quantise_q(0)
-        kb_col = reuse.tile([P, PACK], F32, name="kb_col", offset=AT_Q)
-        nc.vector.tensor_copy(kb_col[:], kb_turned[:, :, ROW])
         nc.vector.tensor_copy(k_first[:], halves_of_words[:, 0 : PASSES * P : PASSES])
+        quantise_q(0)
         nc.vector.tensor_copy(k_rest[:], halves_of_words[:, PASSES * P :: PASSES])
-        nc.vector.tensor_copy(k_second[:], halves_of_words[:, 1::PASSES])
+        nc.vector.tensor_copy(k_second[0][:], halves_of_words[:, 1:N:PASSES])
         quantise_q(1)
+        nc.vector.tensor_copy(k_second[1][:], halves_of_words[:, N + 1 :: PASSES])
 
-        vs_picked = reuse.tile([P, N], F32, name="vs_picked", offset=AT_Q + 4 * N)
-        nc.scalar.activation(vs_picked[:, : 16 * VS_SPLIT], vs_pool[:].indirect(offsets[:, :VS_SPLIT]), ACT.Copy)
-        nc.vector.tensor_copy(vs_picked[:, 16 * VS_SPLIT :], vs_pool[:].indirect(offsets[:, VS_SPLIT:]))
-        vs_col = sb.tile([P, PACK, 1], F32, name="vs_col")
-        nc.sync.dma_start(vs_col[:, :, 0], vs_picked[ROW:, :].rearrange("r (p t) -> r p t", t=PACK))
+        kb_col = reuse.tile([P, PACK], F32, name="kb_col", offset=AT_Q + 8 * N - 64)
+        nc.scalar.copy(kb_col[:], kb_turned[:, :, ROW])
+        vs_picked = reuse.tile([P, PACK, P], F32, name="vs_picked", offset=AT_Q + 4 * N - 64)
+        nc.vector.tensor_copy(
+            by_place(vs_picked[:].bitcast(U32))[:, : 4 * VS_SPLIT], vs_pool[:].bitcast(U32).indirect(offsets[:, :VS_SPLIT])
+        )
+        vs_listed = reuse.tile([P, P - 4 * VS_SPLIT, PACK], F32, name="vs_listed", offset=AT_Q + 8 * N - 32)
+        nc.scalar.activation(vs_listed[:].rearrange("p m t -> p (m t)"), vs_pool[:].indirect(offsets[:, VS_SPLIT:]), ACT.Copy)
+        nc.scalar.copy(vs_picked[:, :, 4 * VS_SPLIT :], vs_listed[:].rearrange("p m t -> p t m"))
 
         p_all = sb.tile([P, PACK, NQ], F32, name="p_all", tag="p_then_value_codes", align_bytes=64)
         acc = [ps.tile([P, NQ], F32, name="scores%d" % t, tag="bank%d" % t) for t in range(PACK)]
@@ -145,6 +149,10 @@ def tile_attend_silu_kb_topkq128n512t2048_kernel(tc, qT, k_words, k_scales, vT, 
                 )
         for t in range(PACK):
             nc.scalar.activation(p_all[:, t, :], acc[t][:], ACT.Silu, bias=kb_col[:, t : t + 1])
+
+        vs_turned = ps.tile([P, PACK, P], F32, name="vs_turned")
+        for t in range(PACK):
+            nc.tensor.transpose(vs_turned[:, t, :], vs_picked[:, t, :], ident[:])
 
         v_picked = sb.tile([P, 2, P, 2], BF16, name="v_picked")
         v_slots = v_picked[:].rearrange("p u m e -> p m u e")
@@ -168,7 +176,7 @@ def tile_attend_silu_kb_topkq128n512t2048_kernel(tc, qT, k_words, k_scales, vT, 
             nc.vector.tensor_tensor(
                 w_bf[:, rows].rearrange("p (c i) t -> p c t i", i=4),
                 p_all[:, :, rows].rearrange("p t (c i) -> p c t i", i=4),
-                vs_col[:].unsqueeze(1).to_broadcast([P, NQ // 8, PACK, 4]),
+                vs_turned[:, :, ROW:].unsqueeze(1).to_broadcast([P, NQ // 8, PACK, 4]),
                 MULT,
             )
         for rows in halves:

from contextlib import ExitStack

import concourse.mybir as mybir
from concourse.masks import make_identity

D, T, N, NQ, DV = 1024, 2048, 512, 128, 128
FLOPS = 2 * NQ * N * (D + DV)
BYTES = 4 * D * NQ + 4 * 128 * T + 2 * 16 * T + 4 * DV * T + 2 * 4 * T + 2 * 128 * (N // 16) + 4 * NQ * DV

F32 = mybir.dt.float32
BF16 = mybir.dt.bfloat16
I32 = mybir.dt.int32
U32 = mybir.dt.uint32
U16 = mybir.dt.uint16
U8 = mybir.dt.uint8
FP8X4 = mybir.dt.float8_e4m3fn_x4
FP4X4 = mybir.dt.float4_e2m1fn_x4
ACT = mybir.ActivationFunctionType
MULT = mybir.AluOpType.mult

P = 128
PACK = 4
PASSES = D // (P * PACK)
ROW = 127
SCALE_ROWS = 32
HALF = DV // 2
VS_HEAD = 256
VS_TAIL = 1280
VS_OVERLAP = 8
V_EARLY = T // 4
VS_SPLIT = 24
V_SPLIT = 24
AT_SCALE = 0
AT_V = AT_SCALE + T
AT_WORDS = AT_V + 4 * T
AT_Q = AT_WORDS + 4 * T


def by_place(ap):
    return ap.rearrange("p t m -> p m t")


def tile_attend_silu_kb_topkq128n512t2048_kernel(tc, qT, k_words, k_scales, vT, vs, kb, offs, out):
    nc = tc.nc
    with ExitStack() as ctx:
        sb = ctx.enter_context(tc.tile_pool(name="sb", bufs=1))
        reuse = ctx.enter_context(tc.tile_pool(name="reuse", bufs=1))
        ps = ctx.enter_context(tc.psum_pool(name="ps", bufs=1))

        offsets = sb.tile([P, N // 16], U16, name="offsets")
        scale_pool = reuse.tile([P, T], U8, name="scale_pool", align_bytes=256, offset=AT_SCALE)
        nc.sync.dma_start(scale_pool[:SCALE_ROWS, :].bitcast(I32), k_scales.rearrange("o f t -> f o t").bitcast(I32))
        nc.sync.dma_start(offsets[:], offs)
        kb_pool = sb.tile([P, T], F32, name="kb_pool", align_bytes=256)
        vs_pool = sb.tile([P, T], F32, name="vs_pool", align_bytes=256)
        nc.scalar.dma_start(kb_pool[ROW:, :], kb[0:1, :])
        nc.scalar.dma_start(vs_pool[ROW:, :], vs[0:1, :])

        word_pool = reuse.tile([P, T], I32, name="word_pool", align_bytes=256, offset=AT_WORDS)
        nc.sync.dma_start(word_pool[:], k_words[0].rearrange("p t b -> p (t b)").bitcast(I32))
        q_raw = [reuse.tile([P, PACK, NQ], F32, name="q_raw%d" % o, align_bytes=256, offset=AT_Q + o * 4 * N) for o in range(PASSES)]
        for o in range(PASSES):
            nc.sync.dma_start(q_raw[o][:], qT[0].rearrange("(o p t) n -> p o t n", o=PASSES, t=PACK)[:, o])
        v_pool = reuse.tile([P, T], F32, name="v_pool", align_bytes=256, offset=AT_V)
        nc.sync.dma_start(v_pool[:, :V_EARLY], vT[:, :V_EARLY])

        ident = sb.tile([P, P], F32, name="ident")
        nc.vector.memset(ident[:], 0.0)
        make_identity(nc, ident[:], nomemset=True)
        nc.vector.memset(scale_pool[32:64, :].bitcast(I32), 0)
        nc.vector.memset(scale_pool[64:, :].bitcast(I32), 0)
        warm_in = sb.tile([P, 1], F32, name="warm_in")
        nc.vector.memset(warm_in[:], 0.0)
        nc.vector.memset(kb_pool[:ROW, :].bitcast(I32), 0)
        nc.vector.memset(vs_pool[:ROW, :VS_HEAD].bitcast(I32), 0)
        nc.gpsimd.memset(vs_pool[:ROW, VS_HEAD - VS_OVERLAP : VS_TAIL].bitcast(I32), 0)
        warm_out = sb.tile([P, 1], F32, name="warm_out")
        nc.scalar.activation(warm_out[:], warm_in[:], ACT.Silu)

        scale_picked = sb.tile([P, PACK, P], U8, name="scale_picked", align_bytes=256)
        nc.vector.tensor_copy(by_place(scale_picked[:]), scale_pool[:].indirect(offsets[:]))
        planes = reuse.tile([P, PASSES, N], U8, name="planes", align_bytes=256, offset=AT_SCALE)
        for quad in (0, 2, 1, 3):
            nc.sync.dma_start(
                planes[32 * quad : 32 * quad + 4].bitcast(I32),
                scale_picked[8 * quad : 8 * quad + 8].rearrange("p t m -> p (t m)").bitcast(I32),
            )
        nc.sync.dma_start(v_pool[:, V_EARLY:], vT[:, V_EARLY:])
        nc.vector.memset(vs_pool[:ROW, VS_TAIL:].bitcast(I32), 0)

        kb_picked = sb.tile([P, N], F32, name="kb_picked")
        nc.scalar.activation(kb_picked[:], kb_pool[:].indirect(offsets[:]), ACT.Copy)
        kb_turned = ps.tile([P, PACK, P], F32, name="kb_turned", tag="kb_then_y")
        for t in range(PACK):
            nc.tensor.transpose(kb_turned[:, t, :], kb_picked[:, t::PACK], ident[:])

        words = sb.tile([P, PACK, P], U32, name="words")
        nc.vector.tensor_copy(by_place(words[:]), word_pool[:].bitcast(U32).indirect(offsets[:]))

        q_bf = [sb.tile([P, NQ, PACK], BF16, name="q_bf%d" % o, align_bytes=64) for o in range(PASSES)]
        q_codes = [reuse.tile([P, NQ], U32, name="q_codes%d" % o, align_bytes=64, offset=AT_WORDS + o * 4 * NQ) for o in range(PASSES)]
        q_scale = [sb.tile([P, NQ], U8, name="q_scale%d" % o, align_bytes=64) for o in range(PASSES)]
        k_first = sb.tile([P, P], U16, name="k_first", align_bytes=64)
        k_rest = sb.tile([P, N - P], U16, name="k_rest", align_bytes=64)
        k_second = [sb.tile([P, N // 2], U16, name="k_second%d" % h, align_bytes=64) for h in range(2)]
        k_codes = [
            [k_first[:]] + [k_rest[:, t * P : (t + 1) * P] for t in range(PACK - 1)],
            [k_second[t // 2][:, t % 2 * P : (t % 2 + 1) * P] for t in range(PACK)],
        ]
        halves_of_words = words[:].rearrange("p t m -> p (t m)").bitcast(U16)

        def quantise_q(o):
            nc.scalar.activation(
                q_bf[o][:].rearrange("p (c i) t -> p c t i", i=4),
                q_raw[o][:].rearrange("p t (c i) -> p c t i", i=4),
                ACT.Copy,
            )
            nc.vector.quantize_mx(out=q_codes[o][:].bitcast(FP8X4), scales=q_scale[o][:], in_=q_bf[o][:].rearrange("p n t -> p (n t)"))

        nc.vector.tensor_copy(k_first[:], halves_of_words[:, 0 : PASSES * P : PASSES])
        quantise_q(0)
        nc.vector.tensor_copy(k_rest[:], halves_of_words[:, PASSES * P :: PASSES])
        nc.vector.tensor_copy(k_second[0][:], halves_of_words[:, 1:N:PASSES])
        quantise_q(1)
        nc.vector.tensor_copy(k_second[1][:], halves_of_words[:, N + 1 :: PASSES])

        kb_col = reuse.tile([P, PACK], F32, name="kb_col", offset=AT_Q + 8 * N - 64)
        nc.scalar.copy(kb_col[:], kb_turned[:, :, ROW])
        vs_picked = reuse.tile([P, PACK, P], F32, name="vs_picked", offset=AT_Q + 4 * N - 64)
        nc.vector.tensor_copy(
            by_place(vs_picked[:].bitcast(U32))[:, : 4 * VS_SPLIT], vs_pool[:].bitcast(U32).indirect(offsets[:, :VS_SPLIT])
        )
        vs_listed = reuse.tile([P, P - 4 * VS_SPLIT, PACK], F32, name="vs_listed", offset=AT_Q + 8 * N - 32)
        nc.scalar.activation(vs_listed[:].rearrange("p m t -> p (m t)"), vs_pool[:].indirect(offsets[:, VS_SPLIT:]), ACT.Copy)
        nc.scalar.copy(vs_picked[:, :, 4 * VS_SPLIT :], vs_listed[:].rearrange("p m t -> p t m"))

        p_all = sb.tile([P, PACK, NQ], F32, name="p_all", tag="p_then_value_codes", align_bytes=64)
        acc = [ps.tile([P, NQ], F32, name="scores%d" % t, tag="bank%d" % t) for t in range(PACK)]
        for o in range(PASSES):
            for t in range(PACK):
                nc.tensor.matmul_mx(
                    out=acc[t][:],
                    lhsT=k_codes[o][t].bitcast(FP4X4),
                    lhsT_scale=planes[:, o, t * P : (t + 1) * P],
                    rhs=q_codes[o][:].bitcast(FP8X4),
                    rhs_scale=q_scale[o][:],
                    start=(o == 0),
                    stop=(o == PASSES - 1),
                )
        for t in range(PACK):
            nc.scalar.activation(p_all[:, t, :], acc[t][:], ACT.Silu, bias=kb_col[:, t : t + 1])

        vs_turned = ps.tile([P, PACK, P], F32, name="vs_turned")
        for t in range(PACK):
            nc.tensor.transpose(vs_turned[:, t, :], vs_picked[:, t, :], ident[:])

        v_picked = sb.tile([P, 2, P, 2], BF16, name="v_picked")
        v_slots = v_picked[:].rearrange("p u m e -> p m u e")
        nc.vector.tensor_copy(v_slots[:, : 4 * V_SPLIT], v_pool[:].indirect(offsets[:, :V_SPLIT]))
        nc.scalar.activation(v_slots[:, 4 * V_SPLIT :], v_pool[:].indirect(offsets[:, V_SPLIT:]), ACT.Copy)
        v_turned = ps.tile([P, 2, DV], F32, name="v_turned")
        for u in range(2):
            nc.tensor.transpose(v_turned[:, u, :], v_picked[:, u].rearrange("p m e -> p (m e)").bitcast(F32), ident[:])
        v_bf = sb.tile([P, DV * PACK], BF16, name="v_bf", align_bytes=64)
        for h in range(2):
            nc.scalar.copy(
                v_bf[:].bitcast(F32).rearrange("p (c u) -> p c u", u=2)[:, h * HALF : (h + 1) * HALF],
                v_turned[:].rearrange("p u c -> p c u")[:, h * HALF : (h + 1) * HALF],
            )

        w_bf = reuse.tile([P, NQ, PACK], BF16, name="w_bf", align_bytes=64, offset=AT_V)
        w_codes = sb.tile([P, NQ], U32, name="w_codes", align_bytes=64)
        w_scale = sb.tile([P, NQ], U8, name="w_scale", align_bytes=64)
        halves = [slice(h * NQ // 2, (h + 1) * NQ // 2) for h in range(2)]
        for rows in halves:
            nc.vector.tensor_tensor(
                w_bf[:, rows].rearrange("p (c i) t -> p c t i", i=4),
                p_all[:, :, rows].rearrange("p t (c i) -> p c t i", i=4),
                vs_turned[:, :, ROW:].unsqueeze(1).to_broadcast([P, NQ // 8, PACK, 4]),
                MULT,
            )
        for rows in halves:
            nc.vector.quantize_mx(
                out=w_codes[:, rows].bitcast(FP8X4), scales=w_scale[:, rows], in_=w_bf[:, rows].rearrange("p q t -> p (q t)")
            )
        v_codes = sb.tile([P, DV], U32, name="v_codes", tag="p_then_value_codes", align_bytes=64)
        v_scale = sb.tile([P, DV], U8, name="v_scale", align_bytes=64)
        y = sb.tile([NQ, DV], F32, name="y")
        y_acc = [ps.tile([NQ, HALF], F32, name="y_acc0", tag="kb_then_y"), ps.tile([NQ, HALF], F32, name="y_acc1")]
        for h in range(2):
            cols = slice(h * HALF, (h + 1) * HALF)
            nc.vector.quantize_mx(
                out=v_codes[:, cols].bitcast(FP8X4),
                scales=v_scale[:, cols],
                in_=v_bf[:, h * HALF * PACK : (h + 1) * HALF * PACK],
            )
            nc.tensor.matmul_mx(
                out=y_acc[h][:],
                lhsT=w_codes[:].bitcast(FP8X4),
                lhsT_scale=w_scale[:],
                rhs=v_codes[:, cols].bitcast(FP8X4),
                rhs_scale=v_scale[:, cols],
                start=True,
                stop=True,
            )
        for h in range(2):
            nc.vector.tensor_scalar_mul(y[:, h * HALF : (h + 1) * HALF], y_acc[h][:], 1.0 / 16.0)
        nc.sync.dma_start(out[0], y[:])
